import numpy as np
import ml_dtypes


def mxq(x, axis, fmt="e4m3"):
    dtype, down = {"e4m3": (ml_dtypes.float8_e4m3fn, 7), "e5m2": (ml_dtypes.float8_e5m2, 14)}[fmt]
    v = np.moveaxis(np.asarray(x, np.float32).astype(ml_dtypes.bfloat16).astype(np.float64), axis, -1)
    blocks = v.reshape(v.shape[:-1] + (-1, 32))
    amax = np.abs(blocks).max(-1, keepdims=True)
    byte = np.maximum(np.where(amax > 0, np.frexp(amax)[1] - 1 + 127, 0) - down, 1)
    scale = np.exp2(byte - 127.0)
    codes = (blocks / scale).astype(np.float32).astype(dtype).astype(np.float64)
    return np.moveaxis((codes * scale).reshape(v.shape), -1, axis)


WIDE = False


def mx_kscale(k):
    if not WIDE:
        return np.ones(k)
    levels = np.array([10, -10, 5, -5, 0])
    if k % 512:
        return np.exp2(np.random.permutation(np.resize(levels, k // 32))).repeat(32)
    a = np.empty((k // 512, 16))
    for p in range(k // 512):
        a[p, :8] = np.random.permutation(np.resize(levels, 8))
        for g in range(8):
            far = levels[np.abs(levels - a[p, g]) >= 10]
            a[p, g + 8] = far[np.random.randint(len(far))]
    return np.exp2(a.ravel()).repeat(32)


def f64(x):
    return np.asarray(x).astype(np.float64)


def striped8(idx):
    return np.concatenate([v.reshape(-1, 16).T for v in idx]).astype(np.uint16)


def unstriped8(offs):
    return np.stack([offs[16 * g:16 * g + 16].T.reshape(-1) for g in range(8)]).astype(np.int64)


E2M1 = np.array([0.0, 0.5, 1.0, 1.5, 2.0, 3.0, 4.0, 6.0, -0.0, -0.5, -1.0, -1.5, -2.0, -3.0, -4.0, -6.0])


def pack_weight(w, fmt):
    k, n = w.shape
    w = f64(np.asarray(w, np.float32).astype(ml_dtypes.bfloat16)).reshape(k // 32, 32, n)
    amax = np.abs(w).max(1)
    if fmt == "e4m3":
        byte = np.frexp(amax)[1] - 1 + 127 - 7
    else:
        mant, ex = np.frexp(amax / 6.0)
        byte = np.where(mant > 0.5, ex, ex - 1) + 127
    byte = np.clip(np.where(amax > 0, byte, 1), 1, 254)
    scaled = (w * np.exp2(127.0 - byte)[:, None, :]).reshape(k, n).astype(np.float32)
    by_word = np.ascontiguousarray(scaled.reshape(k // 512, 128, 4, n).transpose(0, 1, 3, 2))
    if fmt == "e4m3":
        words = by_word.astype(ml_dtypes.float8_e4m3fn).view(np.uint8)
    else:
        c = by_word.astype(ml_dtypes.float4_e2m1fn).view(np.uint8) & 0xF
        words = (c[..., 0::2] | (c[..., 1::2] << 4)).reshape(k // 512, 128, 2 * n)
    return np.ascontiguousarray(words), np.ascontiguousarray(byte.astype(np.uint8).reshape(k // 512, 16, n))


def unpack_weight(words, scales, fmt):
    g, _, n = scales.shape
    words = np.ascontiguousarray(words).reshape(g, 128, n, -1)
    if fmt == "e4m3":
        vals = words.view(ml_dtypes.float8_e4m3fn).astype(np.float64)
    else:
        nib = np.empty((g, 128, n, 4), np.uint8)
        nib[..., 0::2] = words & 0xF
        nib[..., 1::2] = words >> 4
        vals = E2M1[nib]
    vals = vals * np.repeat(np.exp2(scales.astype(np.float64) - 127.0), 8, axis=1)[..., None]
    return vals.transpose(0, 1, 3, 2).reshape(g * 512, n)


K, M, T, S = 512, 512, 2048, 1024


def setup_inputs():
    n = np.random.standard_normal
    s = mx_kscale(K)[:, None]
    p_w = pack_weight(n((K, M)) / np.sqrt(K) / s, "e2m1")
    return {
        "x": (n((K, S)) * s).astype(np.float32),
        "w_words": p_w[0],
        "w_scales": p_w[1],
        "wgo": np.repeat(np.random.uniform(0.5, 2.0, (8, S)), 16, axis=0).astype(np.float32),
        "offs": striped8(np.stack([np.random.permutation(T)[:S] for _ in range(8)])),
    }


def reference(x, w_words, w_scales, wgo, offs):
    x_ = mxq(f64(x), 0, "e4m3")
    w_ = unpack_weight(w_words, w_scales, "e2m1")
    y = w_.T @ x_
    place = unstriped8(offs)[np.arange(M) % 128 // 16]
    out = np.zeros((M, T))
    out[np.arange(M)[:, None], place] = f64(wgo)[np.arange(M) % 128] * (y)
    return out

@@ -1,0 +1,131 @@
+from contextlib import ExitStack
+
+import concourse.mybir as mybir
+
+K, M, T, S = 512, 512, 2048, 1024
+FLOPS = 2 * K * M * S
+
+F32 = mybir.dt.float32
+BF16 = mybir.dt.bfloat16
+I32 = mybir.dt.int32
+U32 = mybir.dt.uint32
+U16 = mybir.dt.uint16
+U8 = mybir.dt.uint8
+FP8X4 = mybir.dt.float8_e4m3fn_x4
+FP4X4 = mybir.dt.float4_e2m1fn_x4
+
+P = 128
+PACK = 4
+BLOCKS = M // P
+HALF = S // 2
+LIST_COLS = HALF // 16
+CHUNK = HALF // 2
+VECTOR_COLS = 160
+WINDOWS = 3
+
+
+def tile_list_hscat_none_kernel(tc, x, w_words, w_scales, wgo, offs, out):
+    nc = tc.nc
+    x_rows = x.rearrange("(p i) j -> p i j", i=PACK)
+
+    with ExitStack() as ctx:
+        keep = ctx.enter_context(tc.tile_pool(name="keep", bufs=1))
+        window_pool = ctx.enter_context(tc.tile_pool(name="window_pool", bufs=WINDOWS))
+        psum = ctx.enter_context(tc.psum_pool(name="psum", bufs=1))
+
+        offsets = keep.tile([P, S // 16], U16, name="offsets")
+        words = keep.tile([P, 2 * M], U8, name="words", align_bytes=64)
+        w_plane = keep.tile([P, M], U8, name="w_plane", align_bytes=64)
+        out_weights = [keep.tile([P, HALF], F32, name=f"out_weights{h}") for h in range(2)]
+        raw_chunks = [keep.tile([P, PACK, CHUNK], F32, name=f"raw_chunk{c}") for c in range(2)]
+        raw_second = keep.tile([P, PACK, HALF], F32, name="raw_second", tag="shared")
+        grouped = [keep.tile([P, HALF, PACK], BF16, name=f"grouped{h}", align_bytes=64) for h in range(2)]
+        codes = [keep.tile([P, HALF], U32, name=f"codes{h}", align_bytes=64) for h in range(2)]
+        x_plane = [keep.tile([P, HALF], U8, name=f"x_plane{h}", align_bytes=64) for h in range(2)]
+        banks = [[psum.tile([P, HALF], F32, name=f"bank{b}{h}") for h in range(2)] for b in range(BLOCKS)]
+        products = {}
+        windows = {}
+
+        nc.gpsimd.memset(w_plane[:].bitcast(I32), 0)
+        nc.sync.dma_start(offsets[:], offs)
+        for c in range(2):
+            nc.sync.dma_start(out=raw_chunks[c][:], in_=x_rows[:, :, CHUNK * c : CHUNK * (c + 1)])
+        for q in range(4):
+            nc.scalar.dma_start(
+                out=w_plane[32 * q : 32 * q + 4, :].bitcast(I32),
+                in_=w_scales[0, 4 * q : 4 * q + 4, :].bitcast(I32),
+            )
+        nc.sync.dma_start(out=words[:].bitcast(I32), in_=w_words[0].bitcast(I32))
+        nc.sync.dma_start(out=out_weights[0][:], in_=wgo[:, 0:HALF])
+        nc.sync.dma_start(out=raw_second[:], in_=x_rows[:, :, HALF:S])
+        nc.sync.dma_start(out=out_weights[1][:], in_=wgo[:, HALF:S])
+
+        def group(engine_copy, raw, raw_c0, half, c0, c1):
+            engine_copy(
+                out=grouped[half][:, c0:c1, :],
+                in_=raw[:, :, c0 - raw_c0 : c1 - raw_c0].rearrange("p i j -> p j i"),
+            )
+
+        def quantize(half, c0, c1):
+            nc.vector.quantize_mx(
+                out=codes[half][:, c0:c1].bitcast(FP8X4),
+                scales=x_plane[half][:, c0:c1],
+                in_=grouped[half][:, c0:c1, :].rearrange("p j i -> p (j i)"),
+            )
+
+        def multiply(b, half, c0, c1):
+            nc.tensor.matmul_mx(
+                out=banks[b][half][:, c0:c1],
+                lhsT=words[:, 2 * P * b : 2 * P * (b + 1)].bitcast(FP4X4),
+                lhsT_scale=w_plane[:, P * b : P * (b + 1)],
+                rhs=codes[half][:, c0:c1].bitcast(FP8X4),
+                rhs_scale=x_plane[half][:, c0:c1],
+                start=True,
+                stop=True,
+            )
+            if c0 == 0:
+                tag = "shared" if (b, half) == (2, 0) else f"product{b}{half}"
+                products[b, half] = keep.tile([P, HALF], F32, name=f"product{b}{half}", tag=tag)
+            nc.scalar.copy(out=products[b, half][:, c0:c1], in_=banks[b][half][:, c0:c1])
+
+        def place(b, half):
+            nc.vector.tensor_tensor(
+                windows[b][:].indirect(offsets[:, LIST_COLS * half : LIST_COLS * (half + 1)]),
+                products[b, half][:],
+                out_weights[half][:],
+                mybir.AluOpType.mult,
+            )
+
+        def store(b):
+            nc.sync.dma_start(out=out[P * b : P * (b + 1), :], in_=windows[b][:])
+
+        for b in range(WINDOWS):
+            windows[b] = window_pool.tile([P, T], F32, name=f"window{b}", tag="window", align_bytes=64)
+            nc.vector.memset(windows[b][:], 0.0)
+
+        for c in range(2):
+            c0, c1 = CHUNK * c, CHUNK * (c + 1)
+            group(nc.vector.tensor_copy, raw_chunks[c], c0, 0, c0, c0 + VECTOR_COLS)
+            group(nc.scalar.copy, raw_chunks[c], c0, 0, c0 + VECTOR_COLS, c1)
+            quantize(0, c0, c1)
+        for c in range(2):
+            multiply(0, 0, CHUNK * c, CHUNK * (c + 1))
+        multiply(1, 0, 0, HALF)
+        place(0, 0)
+
+        group(nc.scalar.copy, raw_second, 0, 1, 0, HALF)
+        multiply(2, 0, 0, HALF)
+        place(1, 0)
+        multiply(3, 0, 0, HALF)
+        quantize(1, 0, HALF)
+        for b in range(BLOCKS):
+            multiply(b, 1, 0, HALF)
+        place(2, 0)
+        for b in range(WINDOWS):
+            place(b, 1)
+            store(b)
+
+        windows[3] = windows[0]
+        for half in range(2):
+            place(3, half)
+        store(3)

@@ -17,10 +17,10 @@ FP4X4 = mybir.dt.float4_e2m1fn_x4
 P = 128
 PACK = 4
 BLOCKS = M // P
-HALF = S // 2
-LIST_COLS = HALF // 16
-CHUNK = HALF // 2
-VECTOR_COLS = 160
+BANK = 512
+STRIPE = 16
+EDGES = (0, 128, 256, 512, 1024)
+GROUP_COLS = 128
 WINDOWS = 3
 
 
@@ -30,102 +30,107 @@ def tile_list_hscat_none_kernel(tc, x, w_words, w_scales, wgo, offs, out):
 
     with ExitStack() as ctx:
         keep = ctx.enter_context(tc.tile_pool(name="keep", bufs=1))
-        window_pool = ctx.enter_context(tc.tile_pool(name="window_pool", bufs=WINDOWS))
         psum = ctx.enter_context(tc.psum_pool(name="psum", bufs=1))
 
-        offsets = keep.tile([P, S // 16], U16, name="offsets")
+        offsets = keep.tile([P, S // STRIPE], U16, name="offsets")
         words = keep.tile([P, 2 * M], U8, name="words", align_bytes=64)
         w_plane = keep.tile([P, M], U8, name="w_plane", align_bytes=64)
-        out_weights = [keep.tile([P, HALF], F32, name=f"out_weights{h}") for h in range(2)]
-        raw_chunks = [keep.tile([P, PACK, CHUNK], F32, name=f"raw_chunk{c}") for c in range(2)]
-        raw_second = keep.tile([P, PACK, HALF], F32, name="raw_second", tag="shared")
-        grouped = [keep.tile([P, HALF, PACK], BF16, name=f"grouped{h}", align_bytes=64) for h in range(2)]
-        codes = [keep.tile([P, HALF], U32, name=f"codes{h}", align_bytes=64) for h in range(2)]
-        x_plane = [keep.tile([P, HALF], U8, name=f"x_plane{h}", align_bytes=64) for h in range(2)]
-        banks = [[psum.tile([P, HALF], F32, name=f"bank{b}{h}") for h in range(2)] for b in range(BLOCKS)]
-        products = {}
-        windows = {}
+        out_weights = keep.tile([P, S], F32, name="out_weights")
+        raw = [
+            keep.tile([P, PACK, EDGES[c + 1] - EDGES[c]], F32, name=f"raw{c}", tag=f"raw{c}", align_bytes=64) for c in range(len(EDGES) - 1)
+        ]
+        grouped = {}
+        codes = keep.tile([P, S], U32, name="codes", align_bytes=64)
+        x_plane = keep.tile([P, S], U8, name="x_plane", align_bytes=64)
+        banks = [[psum.tile([P, BANK], F32, name=f"bank{b}{h}") for h in range(2)] for b in range(BLOCKS)]
+        windows = [keep.tile([P, T], F32, name=f"window{b}", align_bytes=64) for b in range(WINDOWS)]
 
-        nc.gpsimd.memset(w_plane[:].bitcast(I32), 0)
+        def load_x(c):
+            nc.sync.dma_start(out=raw[c][:], in_=x_rows[:, :, EDGES[c] : EDGES[c + 1]])
+
+        nc.vector.memset(w_plane[:].bitcast(I32), 0)
         nc.sync.dma_start(offsets[:], offs)
-        for c in range(2):
-            nc.sync.dma_start(out=raw_chunks[c][:], in_=x_rows[:, :, CHUNK * c : CHUNK * (c + 1)])
+        load_x(0)
         for q in range(4):
             nc.scalar.dma_start(
                 out=w_plane[32 * q : 32 * q + 4, :].bitcast(I32),
                 in_=w_scales[0, 4 * q : 4 * q + 4, :].bitcast(I32),
             )
         nc.sync.dma_start(out=words[:].bitcast(I32), in_=w_words[0].bitcast(I32))
-        nc.sync.dma_start(out=out_weights[0][:], in_=wgo[:, 0:HALF])
-        nc.sync.dma_start(out=raw_second[:], in_=x_rows[:, :, HALF:S])
-        nc.sync.dma_start(out=out_weights[1][:], in_=wgo[:, HALF:S])
+        load_x(1)
+        nc.sync.dma_start(out=out_weights[:, 0:256], in_=wgo[:, 0:256])
+        load_x(2)
+        load_x(3)
+        nc.sync.dma_start(out=out_weights[:, 256:S], in_=wgo[:, 256:S])
 
-        def group(engine_copy, raw, raw_c0, half, c0, c1):
-            engine_copy(
-                out=grouped[half][:, c0:c1, :],
-                in_=raw[:, :, c0 - raw_c0 : c1 - raw_c0].rearrange("p i j -> p j i"),
-            )
+        for b in range(WINDOWS):
+            (nc.vector if b == 0 else nc.gpsimd).memset(windows[b][:].bitcast(I32), 0)
 
-        def quantize(half, c0, c1):
+        def prepare(c, tag=None):
+            width = EDGES[c + 1] - EDGES[c]
+            grouped[c] = keep.tile([P, width * PACK], BF16, name=f"grouped{c}", tag=tag or f"grouped{c}", align_bytes=64)
+            for c0 in range(0, width, GROUP_COLS):
+                nc.scalar.copy(
+                    out=grouped[c][:, PACK * c0 : PACK * (c0 + GROUP_COLS)].rearrange("p (j i) -> p j i", i=PACK),
+                    in_=raw[c][:, :, c0 : c0 + GROUP_COLS].rearrange("p i j -> p j i"),
+                )
             nc.vector.quantize_mx(
-                out=codes[half][:, c0:c1].bitcast(FP8X4),
-                scales=x_plane[half][:, c0:c1],
-                in_=grouped[half][:, c0:c1, :].rearrange("p j i -> p (j i)"),
+                out=codes[:, EDGES[c] : EDGES[c + 1]].bitcast(FP8X4),
+                scales=x_plane[:, EDGES[c] : EDGES[c + 1]],
+                in_=grouped[c][:],
             )
 
-        def multiply(b, half, c0, c1):
+        def multiply(b, c0, c1):
             nc.tensor.matmul_mx(
-                out=banks[b][half][:, c0:c1],
+                out=banks[b][c0 // BANK][:, c0 % BANK : c0 % BANK + c1 - c0],
                 lhsT=words[:, 2 * P * b : 2 * P * (b + 1)].bitcast(FP4X4),
                 lhsT_scale=w_plane[:, P * b : P * (b + 1)],
-                rhs=codes[half][:, c0:c1].bitcast(FP8X4),
-                rhs_scale=x_plane[half][:, c0:c1],
+                rhs=codes[:, c0:c1].bitcast(FP8X4),
+                rhs_scale=x_plane[:, c0:c1],
                 start=True,
                 stop=True,
             )
-            if c0 == 0:
-                tag = "shared" if (b, half) == (2, 0) else f"product{b}{half}"
-                products[b, half] = keep.tile([P, HALF], F32, name=f"product{b}{half}", tag=tag)
-            nc.scalar.copy(out=products[b, half][:, c0:c1], in_=banks[b][half][:, c0:c1])
 
-        def place(b, half):
+        def place(b, c0, c1, tag=None):
+            sums = keep.tile([P, c1 - c0], F32, name=f"sums{b}_{c0}", tag=tag or f"sums{b}_{c0}", align_bytes=64)
+            for h in range(c0 // BANK, (c1 - 1) // BANK + 1):
+                lo, hi = max(c0, BANK * h), min(c1, BANK * (h + 1))
+                nc.scalar.copy(out=sums[:, lo - c0 : hi - c0], in_=banks[b][h][:, lo - BANK * h : hi - BANK * h])
             nc.vector.tensor_tensor(
-                windows[b][:].indirect(offsets[:, LIST_COLS * half : LIST_COLS * (half + 1)]),
-                products[b, half][:],
-                out_weights[half][:],
+                windows[b % WINDOWS][:].indirect(offsets[:, c0 // STRIPE : c1 // STRIPE]),
+                sums[:],
+                out_weights[:, c0:c1],
                 mybir.AluOpType.mult,
             )
 
         def store(b):
-            nc.sync.dma_start(out=out[P * b : P * (b + 1), :], in_=windows[b][:])
+            nc.sync.dma_start(out=out[P * b : P * (b + 1), :], in_=windows[b % WINDOWS][:])
 
+        prepare(0)
+        multiply(0, 0, 128)
+        multiply(1, 0, 128)
+        place(0, 0, 128)
+        prepare(1)
+        place(1, 0, 128, tag="raw1")
+        multiply(0, 128, 256)
+        multiply(2, 0, 256)
+        multiply(1, 128, 256)
+        place(0, 128, 256)
+        prepare(2, tag="sums0_0")
+        place(2, 0, 256, tag="raw2")
         for b in range(WINDOWS):
-            windows[b] = window_pool.tile([P, T], F32, name=f"window{b}", tag="window", align_bytes=64)
-            nc.vector.memset(windows[b][:], 0.0)
-
-        for c in range(2):
-            c0, c1 = CHUNK * c, CHUNK * (c + 1)
-            group(nc.vector.tensor_copy, raw_chunks[c], c0, 0, c0, c0 + VECTOR_COLS)
-            group(nc.scalar.copy, raw_chunks[c], c0, 0, c0 + VECTOR_COLS, c1)
-            quantize(0, c0, c1)
-        for c in range(2):
-            multiply(0, 0, CHUNK * c, CHUNK * (c + 1))
-        multiply(1, 0, 0, HALF)
-        place(0, 0)
-
-        group(nc.scalar.copy, raw_second, 0, 1, 0, HALF)
-        multiply(2, 0, 0, HALF)
-        place(1, 0)
-        multiply(3, 0, 0, HALF)
-        quantize(1, 0, HALF)
+            multiply(b, 256, 512)
+        multiply(3, 0, 512)
+        place(0, 256, 512)
+        prepare(3)
+        place(1, 128, 512, tag="raw3")
         for b in range(BLOCKS):
-            multiply(b, 1, 0, HALF)
-        place(2, 0)
-        for b in range(WINDOWS):
-            place(b, 1)
-            store(b)
-
-        windows[3] = windows[0]
-        for half in range(2):
-            place(3, half)
+            multiply(b, 512, S)
+        place(0, 512, S)
+        store(0)
+        place(1, 512, S)
+        store(1)
+        place(2, 256, S)
+        store(2)
+        place(3, 0, S)
         store(3)

@@ -64,7 +64,7 @@ def tile_list_hscat_none_kernel(tc, x, w_words, w_scales, wgo, offs, out):
         nc.sync.dma_start(out=out_weights[:, 256:S], in_=wgo[:, 256:S])
 
         for b in range(WINDOWS):
-            (nc.vector if b == 0 else nc.gpsimd).memset(windows[b][:].bitcast(I32), 0)
+            nc.vector.memset(windows[b][:].bitcast(I32), 0)
 
         def prepare(c, tag=None):
             width = EDGES[c + 1] - EDGES[c]
@@ -122,7 +122,7 @@ def tile_list_hscat_none_kernel(tc, x, w_words, w_scales, wgo, offs, out):
             multiply(b, 256, 512)
         multiply(3, 0, 512)
         place(0, 256, 512)
-        prepare(3)
+        prepare(3, tag="sums0_128")
         place(1, 128, 512, tag="raw3")
         for b in range(BLOCKS):
             multiply(b, 512, S)

@@ -108,13 +108,12 @@ def tile_list_hscat_none_kernel(tc, x, w_words, w_scales, wgo, offs, out):
 
         prepare(0)
         multiply(0, 0, 128)
-        multiply(1, 0, 128)
         place(0, 0, 128)
         prepare(1)
-        place(1, 0, 128, tag="raw1")
+        multiply(1, 0, 256)
         multiply(0, 128, 256)
         multiply(2, 0, 256)
-        multiply(1, 128, 256)
+        place(1, 0, 256)
         place(0, 128, 256)
         prepare(2, tag="sums0_0")
         place(2, 0, 256, tag="raw2")
@@ -123,7 +122,7 @@ def tile_list_hscat_none_kernel(tc, x, w_words, w_scales, wgo, offs, out):
         multiply(3, 0, 512)
         place(0, 256, 512)
         prepare(3, tag="sums0_128")
-        place(1, 128, 512, tag="raw3")
+        place(1, 256, 512, tag="raw3")
         for b in range(BLOCKS):
             multiply(b, 512, S)
         place(0, 512, S)

@@ -19,7 +19,7 @@ PACK = 4
 BLOCKS = M // P
 BANK = 512
 STRIPE = 16
-EDGES = (0, 128, 256, 512, 1024)
+EDGES = (0, 128, 256, 512, 768, 1024)
 GROUP_COLS = 128
 WINDOWS = 3
 
@@ -32,18 +32,17 @@ def tile_list_hscat_none_kernel(tc, x, w_words, w_scales, wgo, offs, out):
         keep = ctx.enter_context(tc.tile_pool(name="keep", bufs=1))
         psum = ctx.enter_context(tc.psum_pool(name="psum", bufs=1))
 
+        def tile(name, shape, dtype, slot=None):
+            return keep.tile(shape, dtype, name=name, tag=slot or name, align_bytes=64)
+
         offsets = keep.tile([P, S // STRIPE], U16, name="offsets")
-        words = keep.tile([P, 2 * M], U8, name="words", align_bytes=64)
-        w_plane = keep.tile([P, M], U8, name="w_plane", align_bytes=64)
-        out_weights = keep.tile([P, S], F32, name="out_weights")
-        raw = [
-            keep.tile([P, PACK, EDGES[c + 1] - EDGES[c]], F32, name=f"raw{c}", tag=f"raw{c}", align_bytes=64) for c in range(len(EDGES) - 1)
-        ]
-        grouped = {}
-        codes = keep.tile([P, S], U32, name="codes", align_bytes=64)
-        x_plane = keep.tile([P, S], U8, name="x_plane", align_bytes=64)
+        words = tile("words", [P, 2 * M], U8)
+        w_plane = tile("w_plane", [P, M], U8)
+        out_weights = tile("out_weights", [P, S], F32)
+        raw = [tile(f"raw{c}", [P, PACK, EDGES[c + 1] - EDGES[c]], F32) for c in range(len(EDGES) - 1)]
+        x_plane = tile("x_plane", [P, S], U8)
         banks = [[psum.tile([P, BANK], F32, name=f"bank{b}{h}") for h in range(2)] for b in range(BLOCKS)]
-        windows = [keep.tile([P, T], F32, name=f"window{b}", align_bytes=64) for b in range(WINDOWS)]
+        windows = [tile(f"window{b}", [P, T], F32) for b in range(WINDOWS)]
 
         def load_x(c):
             nc.sync.dma_start(out=raw[c][:], in_=x_rows[:, :, EDGES[c] : EDGES[c + 1]])
@@ -62,40 +61,43 @@ def tile_list_hscat_none_kernel(tc, x, w_words, w_scales, wgo, offs, out):
         load_x(2)
         load_x(3)
         nc.sync.dma_start(out=out_weights[:, 256:S], in_=wgo[:, 256:S])
+        load_x(4)
 
         for b in range(WINDOWS):
-            nc.vector.memset(windows[b][:].bitcast(I32), 0)
+            nc.vector.memset(windows[b][:], 0.0)
 
-        def prepare(c, tag=None):
-            width = EDGES[c + 1] - EDGES[c]
-            grouped[c] = keep.tile([P, width * PACK], BF16, name=f"grouped{c}", tag=tag or f"grouped{c}", align_bytes=64)
-            for c0 in range(0, width, GROUP_COLS):
+        def prepare(c, codes, codes_c0, slot=None):
+            c0, c1 = EDGES[c], EDGES[c + 1]
+            grouped = tile(f"grouped{c}", [P, (c1 - c0) * PACK], BF16, slot)
+            for j in range(0, c1 - c0, GROUP_COLS):
                 nc.scalar.copy(
-                    out=grouped[c][:, PACK * c0 : PACK * (c0 + GROUP_COLS)].rearrange("p (j i) -> p j i", i=PACK),
-                    in_=raw[c][:, :, c0 : c0 + GROUP_COLS].rearrange("p i j -> p j i"),
+                    out=grouped[:, PACK * j : PACK * (j + GROUP_COLS)].rearrange("p (j i) -> p j i", i=PACK),
+                    in_=raw[c][:, :, j : j + GROUP_COLS].rearrange("p i j -> p j i"),
                 )
             nc.vector.quantize_mx(
-                out=codes[:, EDGES[c] : EDGES[c + 1]].bitcast(FP8X4),
-                scales=x_plane[:, EDGES[c] : EDGES[c + 1]],
-                in_=grouped[c][:],
+                out=codes[:, c0 - codes_c0 : c1 - codes_c0].bitcast(FP8X4),
+                scales=x_plane[:, c0:c1],
+                in_=grouped[:],
             )
 
-        def multiply(b, c0, c1):
+        def multiply(b, c0, c1, codes, codes_c0, bank=None):
+            bank = banks[b][c0 // BANK] if bank is None else bank
             nc.tensor.matmul_mx(
-                out=banks[b][c0 // BANK][:, c0 % BANK : c0 % BANK + c1 - c0],
+                out=bank[:, c0 % BANK : c0 % BANK + c1 - c0],
                 lhsT=words[:, 2 * P * b : 2 * P * (b + 1)].bitcast(FP4X4),
                 lhsT_scale=w_plane[:, P * b : P * (b + 1)],
-                rhs=codes[:, c0:c1].bitcast(FP8X4),
+                rhs=codes[:, c0 - codes_c0 : c1 - codes_c0].bitcast(FP8X4),
                 rhs_scale=x_plane[:, c0:c1],
                 start=True,
                 stop=True,
             )
 
-        def place(b, c0, c1, tag=None):
-            sums = keep.tile([P, c1 - c0], F32, name=f"sums{b}_{c0}", tag=tag or f"sums{b}_{c0}", align_bytes=64)
+        def place(b, c0, c1, slot=None, bank=None):
+            sums = tile(f"sums{b}_{c0}", [P, c1 - c0], F32, slot)
             for h in range(c0 // BANK, (c1 - 1) // BANK + 1):
                 lo, hi = max(c0, BANK * h), min(c1, BANK * (h + 1))
-                nc.scalar.copy(out=sums[:, lo - c0 : hi - c0], in_=banks[b][h][:, lo - BANK * h : hi - BANK * h])
+                source = banks[b][h] if bank is None else bank
+                nc.scalar.copy(out=sums[:, lo - c0 : hi - c0], in_=source[:, lo - BANK * h : hi - BANK * h])
             nc.vector.tensor_tensor(
                 windows[b % WINDOWS][:].indirect(offsets[:, c0 // STRIPE : c1 // STRIPE]),
                 sums[:],
@@ -106,30 +108,38 @@ def tile_list_hscat_none_kernel(tc, x, w_words, w_scales, wgo, offs, out):
         def store(b):
             nc.sync.dma_start(out=out[P * b : P * (b + 1), :], in_=windows[b % WINDOWS][:])
 
-        prepare(0)
-        multiply(0, 0, 128)
-        place(0, 0, 128)
-        prepare(1)
-        multiply(1, 0, 256)
-        multiply(0, 128, 256)
-        multiply(2, 0, 256)
+        codes_first = tile("codes_first", [P, 256], U32)
+        prepare(0, codes_first, 0)
+        multiply(0, 0, 128, codes_first, 0, bank=banks[0][1])
+        place(0, 0, 128, bank=banks[0][1])
+        prepare(1, codes_first, 0)
+        multiply(1, 0, 256, codes_first, 0)
+        multiply(0, 128, 256, codes_first, 0)
+        multiply(2, 0, 256, codes_first, 0)
+        multiply(3, 0, 256, codes_first, 0)
         place(1, 0, 256)
         place(0, 128, 256)
-        prepare(2, tag="sums0_0")
-        place(2, 0, 256, tag="raw2")
-        for b in range(WINDOWS):
-            multiply(b, 256, 512)
-        multiply(3, 0, 512)
-        place(0, 256, 512)
-        prepare(3, tag="sums0_128")
-        place(1, 256, 512, tag="raw3")
+
+        codes_second = tile("codes_second", [P, 256], U32)
+        prepare(2, codes_second, 256, slot="codes_first")
+        place(2, 0, 256, slot="raw2")
         for b in range(BLOCKS):
-            multiply(b, 512, S)
+            multiply(b, 256, 512, codes_second, 256)
+
+        codes_third = tile("codes_third", [P, 512], U32)
+        prepare(3, codes_third, 512, slot="codes_first")
+        place(0, 256, 512)
+        multiply(0, 512, 768, codes_third, 512)
+        prepare(4, codes_third, 512, slot="codes_second")
+        place(1, 256, 512, slot="raw4")
+        multiply(0, 768, S, codes_third, 512)
+        for b in range(1, BLOCKS):
+            multiply(b, 512, S, codes_third, 512)
         place(0, 512, S)
         store(0)
         place(1, 512, S)
         store(1)
-        place(2, 256, S)
+        place(2, 256, S, slot="codes_second")
         store(2)
-        place(3, 0, S)
+        place(3, 0, S, slot="raw4")
         store(3)

@@ -19,8 +19,9 @@ PACK = 4
 BLOCKS = M // P
 BANK = 512
 STRIPE = 16
-EDGES = (0, 128, 256, 512, 768, 1024)
+EDGES = (0, 128, 256, 512, 1024)
 GROUP_COLS = 128
+LINE = 4
 WINDOWS = 3
 
 
@@ -61,7 +62,6 @@ def tile_list_hscat_none_kernel(tc, x, w_words, w_scales, wgo, offs, out):
         load_x(2)
         load_x(3)
         nc.sync.dma_start(out=out_weights[:, 256:S], in_=wgo[:, 256:S])
-        load_x(4)
 
         for b in range(WINDOWS):
             nc.vector.memset(windows[b][:], 0.0)
@@ -71,8 +71,8 @@ def tile_list_hscat_none_kernel(tc, x, w_words, w_scales, wgo, offs, out):
             grouped = tile(f"grouped{c}", [P, (c1 - c0) * PACK], BF16, slot)
             for j in range(0, c1 - c0, GROUP_COLS):
                 nc.scalar.copy(
-                    out=grouped[:, PACK * j : PACK * (j + GROUP_COLS)].rearrange("p (j i) -> p j i", i=PACK),
-                    in_=raw[c][:, :, j : j + GROUP_COLS].rearrange("p i j -> p j i"),
+                    out=grouped[:, PACK * j : PACK * (j + GROUP_COLS)].rearrange("p (r j i) -> p r i j", j=LINE, i=PACK),
+                    in_=raw[c][:, :, j : j + GROUP_COLS].rearrange("p i (r j) -> p r i j", j=LINE),
                 )
             nc.vector.quantize_mx(
                 out=codes[:, c0 - codes_c0 : c1 - codes_c0].bitcast(FP8X4),
@@ -114,26 +114,22 @@ def tile_list_hscat_none_kernel(tc, x, w_words, w_scales, wgo, offs, out):
         place(0, 0, 128, bank=banks[0][1])
         prepare(1, codes_first, 0)
         multiply(1, 0, 256, codes_first, 0)
-        multiply(0, 128, 256, codes_first, 0)
         multiply(2, 0, 256, codes_first, 0)
+        multiply(0, 128, 256, codes_first, 0)
         multiply(3, 0, 256, codes_first, 0)
         place(1, 0, 256)
-        place(0, 128, 256)
 
         codes_second = tile("codes_second", [P, 256], U32)
         prepare(2, codes_second, 256, slot="codes_first")
         place(2, 0, 256, slot="raw2")
         for b in range(BLOCKS):
             multiply(b, 256, 512, codes_second, 256)
+        place(0, 128, 512)
 
         codes_third = tile("codes_third", [P, 512], U32)
-        prepare(3, codes_third, 512, slot="codes_first")
-        place(0, 256, 512)
-        multiply(0, 512, 768, codes_third, 512)
-        prepare(4, codes_third, 512, slot="codes_second")
-        place(1, 256, 512, slot="raw4")
-        multiply(0, 768, S, codes_third, 512)
-        for b in range(1, BLOCKS):
+        prepare(3, codes_third, 512, slot="codes_second")
+        place(1, 256, 512, slot="raw3")
+        for b in range(BLOCKS):
             multiply(b, 512, S, codes_third, 512)
         place(0, 512, S)
         store(0)
@@ -141,5 +137,5 @@ def tile_list_hscat_none_kernel(tc, x, w_words, w_scales, wgo, offs, out):
         store(1)
         place(2, 256, S, slot="codes_second")
         store(2)
-        place(3, 0, S, slot="raw4")
+        place(3, 0, S, slot="raw3")
         store(3)

@@ -137,5 +137,5 @@ def tile_list_hscat_none_kernel(tc, x, w_words, w_scales, wgo, offs, out):
         store(1)
         place(2, 256, S, slot="codes_second")
         store(2)
-        place(3, 0, S, slot="raw3")
+        place(3, 0, S, slot="sums1_512")
         store(3)

@@ -51,13 +51,13 @@ def tile_list_hscat_none_kernel(tc, x, w_words, w_scales, wgo, offs, out):
         nc.vector.memset(w_plane[:].bitcast(I32), 0)
         nc.sync.dma_start(offsets[:], offs)
         load_x(0)
+        load_x(1)
         for q in range(4):
-            nc.scalar.dma_start(
+            nc.sync.dma_start(
                 out=w_plane[32 * q : 32 * q + 4, :].bitcast(I32),
                 in_=w_scales[0, 4 * q : 4 * q + 4, :].bitcast(I32),
             )
         nc.sync.dma_start(out=words[:].bitcast(I32), in_=w_words[0].bitcast(I32))
-        load_x(1)
         nc.sync.dma_start(out=out_weights[:, 0:256], in_=wgo[:, 0:256])
         load_x(2)
         load_x(3)
@@ -111,8 +111,8 @@ def tile_list_hscat_none_kernel(tc, x, w_words, w_scales, wgo, offs, out):
         codes_first = tile("codes_first", [P, 256], U32)
         prepare(0, codes_first, 0)
         multiply(0, 0, 128, codes_first, 0, bank=banks[0][1])
-        place(0, 0, 128, bank=banks[0][1])
         prepare(1, codes_first, 0)
+        place(0, 0, 128, slot="raw1", bank=banks[0][1])
         multiply(1, 0, 256, codes_first, 0)
         multiply(2, 0, 256, codes_first, 0)
         multiply(0, 128, 256, codes_first, 0)

@@ -92,11 +92,14 @@ def tile_list_hscat_none_kernel(tc, x, w_words, w_scales, wgo, offs, out):
                 stop=True,
             )
 
-        def place(b, c0, c1, slot=None, bank=None):
+        def place(b, c0, c1, slot=None, bank=None, early=None):
             sums = tile(f"sums{b}_{c0}", [P, c1 - c0], F32, slot)
             for h in range(c0 // BANK, (c1 - 1) // BANK + 1):
                 lo, hi = max(c0, BANK * h), min(c1, BANK * (h + 1))
                 source = banks[b][h] if bank is None else bank
+                if early is not None:
+                    nc.scalar.copy(out=sums[:, 0:128], in_=early[:, 0:128])
+                    lo = 128
                 nc.scalar.copy(out=sums[:, lo - c0 : hi - c0], in_=source[:, lo - BANK * h : hi - BANK * h])
             nc.vector.tensor_tensor(
                 windows[b % WINDOWS][:].indirect(offsets[:, c0 // STRIPE : c1 // STRIPE]),
@@ -111,13 +114,14 @@ def tile_list_hscat_none_kernel(tc, x, w_words, w_scales, wgo, offs, out):
         codes_first = tile("codes_first", [P, 256], U32)
         prepare(0, codes_first, 0)
         multiply(0, 0, 128, codes_first, 0, bank=banks[0][1])
+        multiply(1, 0, 128, codes_first, 0, bank=banks[1][1])
         prepare(1, codes_first, 0)
         place(0, 0, 128, slot="raw1", bank=banks[0][1])
-        multiply(1, 0, 256, codes_first, 0)
+        multiply(1, 128, 256, codes_first, 0)
         multiply(2, 0, 256, codes_first, 0)
         multiply(0, 128, 256, codes_first, 0)
         multiply(3, 0, 256, codes_first, 0)
-        place(1, 0, 256)
+        place(1, 0, 256, early=banks[1][1])
 
         codes_second = tile("codes_second", [P, 256], U32)
         prepare(2, codes_second, 256, slot="codes_first")

@@ -51,12 +51,12 @@ def tile_list_hscat_none_kernel(tc, x, w_words, w_scales, wgo, offs, out):
         nc.vector.memset(w_plane[:].bitcast(I32), 0)
         nc.sync.dma_start(offsets[:], offs)
         load_x(0)
-        load_x(1)
         for q in range(4):
             nc.sync.dma_start(
                 out=w_plane[32 * q : 32 * q + 4, :].bitcast(I32),
                 in_=w_scales[0, 4 * q : 4 * q + 4, :].bitcast(I32),
             )
+        load_x(1)
         nc.sync.dma_start(out=words[:].bitcast(I32), in_=w_words[0].bitcast(I32))
         nc.sync.dma_start(out=out_weights[:, 0:256], in_=wgo[:, 0:256])
         load_x(2)

@@ -49,7 +49,6 @@ def tile_list_hscat_none_kernel(tc, x, w_words, w_scales, wgo, offs, out):
             nc.sync.dma_start(out=raw[c][:], in_=x_rows[:, :, EDGES[c] : EDGES[c + 1]])
 
         nc.vector.memset(w_plane[:].bitcast(I32), 0)
-        nc.sync.dma_start(offsets[:], offs)
         load_x(0)
         for q in range(4):
             nc.sync.dma_start(
@@ -59,6 +58,7 @@ def tile_list_hscat_none_kernel(tc, x, w_words, w_scales, wgo, offs, out):
         load_x(1)
         nc.sync.dma_start(out=words[:].bitcast(I32), in_=w_words[0].bitcast(I32))
         nc.sync.dma_start(out=out_weights[:, 0:256], in_=wgo[:, 0:256])
+        nc.sync.dma_start(offsets[:], offs)
         load_x(2)
         load_x(3)
         nc.sync.dma_start(out=out_weights[:, 256:S], in_=wgo[:, 256:S])

@@ -23,6 +23,7 @@ EDGES = (0, 128, 256, 512, 1024)
 GROUP_COLS = 128
 LINE = 4
 WINDOWS = 3
+CLEAR_EARLY = 1152
 
 
 def tile_list_hscat_none_kernel(tc, x, w_words, w_scales, wgo, offs, out):
@@ -63,8 +64,9 @@ def tile_list_hscat_none_kernel(tc, x, w_words, w_scales, wgo, offs, out):
         load_x(3)
         nc.sync.dma_start(out=out_weights[:, 256:S], in_=wgo[:, 256:S])
 
-        for b in range(WINDOWS):
-            nc.vector.memset(windows[b][:], 0.0)
+        nc.vector.memset(windows[0][:], 0.0)
+        nc.vector.memset(windows[1][:], 0.0)
+        nc.vector.memset(windows[2][:, 0:CLEAR_EARLY], 0.0)
 
         def prepare(c, codes, codes_c0, slot=None):
             c0, c1 = EDGES[c], EDGES[c + 1]
@@ -113,6 +115,7 @@ def tile_list_hscat_none_kernel(tc, x, w_words, w_scales, wgo, offs, out):
 
         codes_first = tile("codes_first", [P, 256], U32)
         prepare(0, codes_first, 0)
+        nc.vector.memset(windows[2][:, CLEAR_EARLY - 8 : T], 0.0)
         multiply(0, 0, 128, codes_first, 0, bank=banks[0][1])
         multiply(1, 0, 128, codes_first, 0, bank=banks[1][1])
         prepare(1, codes_first, 0)

@@ -19,11 +19,11 @@ PACK = 4
 BLOCKS = M // P
 BANK = 512
 STRIPE = 16
+LOADS = (0, 128, 256, 384, 512, 1024)
 EDGES = (0, 128, 256, 512, 1024)
 GROUP_COLS = 128
 LINE = 4
 WINDOWS = 3
-CLEAR_EARLY = 1152
 
 
 def tile_list_hscat_none_kernel(tc, x, w_words, w_scales, wgo, offs, out):
@@ -41,13 +41,13 @@ def tile_list_hscat_none_kernel(tc, x, w_words, w_scales, wgo, offs, out):
         words = tile("words", [P, 2 * M], U8)
         w_plane = tile("w_plane", [P, M], U8)
         out_weights = tile("out_weights", [P, S], F32)
-        raw = [tile(f"raw{c}", [P, PACK, EDGES[c + 1] - EDGES[c]], F32) for c in range(len(EDGES) - 1)]
+        raw = [tile(f"raw{c}", [P, PACK, LOADS[c + 1] - LOADS[c]], F32) for c in range(len(LOADS) - 1)]
         x_plane = tile("x_plane", [P, S], U8)
         banks = [[psum.tile([P, BANK], F32, name=f"bank{b}{h}") for h in range(2)] for b in range(BLOCKS)]
         windows = [tile(f"window{b}", [P, T], F32) for b in range(WINDOWS)]
 
         def load_x(c):
-            nc.sync.dma_start(out=raw[c][:], in_=x_rows[:, :, EDGES[c] : EDGES[c + 1]])
+            nc.sync.dma_start(out=raw[c][:], in_=x_rows[:, :, LOADS[c] : LOADS[c + 1]])
 
         nc.vector.memset(w_plane[:].bitcast(I32), 0)
         load_x(0)
@@ -57,30 +57,40 @@ def tile_list_hscat_none_kernel(tc, x, w_words, w_scales, wgo, offs, out):
                 in_=w_scales[0, 4 * q : 4 * q + 4, :].bitcast(I32),
             )
         load_x(1)
-        nc.sync.dma_start(out=words[:].bitcast(I32), in_=w_words[0].bitcast(I32))
+        nc.sync.dma_start(out=words[:, 0:M].bitcast(I32), in_=w_words[0, :, 0:M].bitcast(I32))
         nc.sync.dma_start(out=out_weights[:, 0:256], in_=wgo[:, 0:256])
         nc.sync.dma_start(offsets[:], offs)
+        nc.sync.dma_start(out=words[:, M : 2 * M].bitcast(I32), in_=w_words[0, :, M : 2 * M].bitcast(I32))
         load_x(2)
         load_x(3)
-        nc.sync.dma_start(out=out_weights[:, 256:S], in_=wgo[:, 256:S])
+        load_x(4)
+        nc.sync.dma_start(out=out_weights[:, 256:1024], in_=wgo[:, 256:1024])
 
-        nc.vector.memset(windows[0][:], 0.0)
-        nc.vector.memset(windows[1][:], 0.0)
-        nc.vector.memset(windows[2][:, 0:CLEAR_EARLY], 0.0)
+        nc.vector.memset(windows[0][:, 0 : T], 0.0)
+        nc.vector.memset(windows[1][:, 0 : T], 0.0)
+        nc.vector.memset(windows[2][:, 0:1536], 0.0)
 
-        def prepare(c, codes, codes_c0, slot=None):
+        def group(grouped, g0, j0, j1, copy):
+            c = max(c for c in range(len(raw)) if LOADS[c] <= j0)
+            copy(
+                out=grouped[:, PACK * (j0 - g0) : PACK * (j1 - g0)].rearrange("p (r j i) -> p r i j", j=LINE, i=PACK),
+                in_=raw[c][:, :, j0 - LOADS[c] : j1 - LOADS[c]].rearrange("p i (r j) -> p r i j", j=LINE),
+            )
+
+        def quantize(c, grouped, codes, codes_c0):
             c0, c1 = EDGES[c], EDGES[c + 1]
-            grouped = tile(f"grouped{c}", [P, (c1 - c0) * PACK], BF16, slot)
-            for j in range(0, c1 - c0, GROUP_COLS):
-                nc.scalar.copy(
-                    out=grouped[:, PACK * j : PACK * (j + GROUP_COLS)].rearrange("p (r j i) -> p r i j", j=LINE, i=PACK),
-                    in_=raw[c][:, :, j : j + GROUP_COLS].rearrange("p i (r j) -> p r i j", j=LINE),
-                )
             nc.vector.quantize_mx(
                 out=codes[:, c0 - codes_c0 : c1 - codes_c0].bitcast(FP8X4),
                 scales=x_plane[:, c0:c1],
                 in_=grouped[:],
             )
+
+        def prepare(c, codes, codes_c0, slot=None):
+            c0, c1 = EDGES[c], EDGES[c + 1]
+            grouped = tile(f"grouped{c}", [P, (c1 - c0) * PACK], BF16, slot)
+            for j in range(c0, c1, GROUP_COLS):
+                group(grouped, c0, j, j + GROUP_COLS, nc.scalar.copy)
+            quantize(c, grouped, codes, codes_c0)
 
         def multiply(b, c0, c1, codes, codes_c0, bank=None):
             bank = banks[b][c0 // BANK] if bank is None else bank
@@ -114,12 +124,16 @@ def tile_list_hscat_none_kernel(tc, x, w_words, w_scales, wgo, offs, out):
             nc.sync.dma_start(out=out[P * b : P * (b + 1), :], in_=windows[b % WINDOWS][:])
 
         codes_first = tile("codes_first", [P, 256], U32)
-        prepare(0, codes_first, 0)
-        nc.vector.memset(windows[2][:, CLEAR_EARLY - 8 : T], 0.0)
+        grouped0 = tile("grouped0", [P, 128 * PACK], BF16)
+        group(grouped0, 0, 0, 128, nc.scalar.copy)
+        quantize(0, grouped0, codes_first, 0)
         multiply(0, 0, 128, codes_first, 0, bank=banks[0][1])
         multiply(1, 0, 128, codes_first, 0, bank=banks[1][1])
-        prepare(1, codes_first, 0)
-        place(0, 0, 128, slot="raw1", bank=banks[0][1])
+        grouped1 = tile("grouped1", [P, 128 * PACK], BF16)
+        group(grouped1, 128, 128, 256, nc.vector.tensor_copy)
+        nc.vector.memset(windows[2][:, 1528 : T], 0.0)
+        quantize(1, grouped1, codes_first, 0)
+        place(0, 0, 128, bank=banks[0][1])
         multiply(1, 128, 256, codes_first, 0)
         multiply(2, 0, 256, codes_first, 0)
         multiply(0, 128, 256, codes_first, 0)
@@ -128,14 +142,14 @@ def tile_list_hscat_none_kernel(tc, x, w_words, w_scales, wgo, offs, out):
 
         codes_second = tile("codes_second", [P, 256], U32)
         prepare(2, codes_second, 256, slot="codes_first")
-        place(2, 0, 256, slot="raw2")
+        place(2, 0, 256, slot="raw3")
         for b in range(BLOCKS):
             multiply(b, 256, 512, codes_second, 256)
         place(0, 128, 512)
 
         codes_third = tile("codes_third", [P, 512], U32)
         prepare(3, codes_third, 512, slot="codes_second")
-        place(1, 256, 512, slot="raw3")
+        place(1, 256, 512, slot="raw4")
         for b in range(BLOCKS):
             multiply(b, 512, S, codes_third, 512)
         place(0, 512, S)

@@ -24,6 +24,7 @@ EDGES = (0, 128, 256, 512, 1024)
 GROUP_COLS = 128
 LINE = 4
 WINDOWS = 3
+STORE_PARTS = (1, 4, 4, 1)
 
 
 def tile_list_hscat_none_kernel(tc, x, w_words, w_scales, wgo, offs, out):
@@ -68,7 +69,7 @@ def tile_list_hscat_none_kernel(tc, x, w_words, w_scales, wgo, offs, out):
 
         nc.vector.memset(windows[0][:, 0 : T], 0.0)
         nc.vector.memset(windows[1][:, 0 : T], 0.0)
-        nc.vector.memset(windows[2][:, 0:1536], 0.0)
+        nc.vector.memset(windows[2][:, 0:896], 0.0)
 
         def group(grouped, g0, j0, j1, copy):
             c = max(c for c in range(len(raw)) if LOADS[c] <= j0)
@@ -121,19 +122,25 @@ def tile_list_hscat_none_kernel(tc, x, w_words, w_scales, wgo, offs, out):
             )
 
         def store(b):
-            nc.sync.dma_start(out=out[P * b : P * (b + 1), :], in_=windows[b % WINDOWS][:])
+            width = T // STORE_PARTS[b]
+            for t in range(0, T, width):
+                nc.sync.dma_start(out=out[P * b : P * (b + 1), t : t + width], in_=windows[b % WINDOWS][:, t : t + width])
 
         codes_first = tile("codes_first", [P, 256], U32)
         grouped0 = tile("grouped0", [P, 128 * PACK], BF16)
-        group(grouped0, 0, 0, 128, nc.scalar.copy)
+        group(grouped0, 0, 0, 64, nc.vector.tensor_copy)
+        group(grouped0, 0, 64, 128, nc.scalar.copy)
+        nc.vector.memset(windows[2][:, 888:1280], 0.0)
         quantize(0, grouped0, codes_first, 0)
+        nc.vector.memset(windows[2][:, 1272:1664], 0.0)
         multiply(0, 0, 128, codes_first, 0, bank=banks[0][1])
         multiply(1, 0, 128, codes_first, 0, bank=banks[1][1])
         grouped1 = tile("grouped1", [P, 128 * PACK], BF16)
-        group(grouped1, 128, 128, 256, nc.vector.tensor_copy)
-        nc.vector.memset(windows[2][:, 1528 : T], 0.0)
+        group(grouped1, 128, 128, 192, nc.vector.tensor_copy)
+        group(grouped1, 128, 192, 256, nc.scalar.copy)
+        nc.vector.memset(windows[2][:, 1656:T], 0.0)
         quantize(1, grouped1, codes_first, 0)
-        place(0, 0, 128, bank=banks[0][1])
+        place(0, 0, 128, slot="raw1", bank=banks[0][1])
         multiply(1, 128, 256, codes_first, 0)
         multiply(2, 0, 256, codes_first, 0)
         multiply(0, 128, 256, codes_first, 0)

@@ -69,7 +69,7 @@ def tile_list_hscat_none_kernel(tc, x, w_words, w_scales, wgo, offs, out):
 
         nc.vector.memset(windows[0][:, 0 : T], 0.0)
         nc.vector.memset(windows[1][:, 0 : T], 0.0)
-        nc.vector.memset(windows[2][:, 0:896], 0.0)
+        nc.vector.memset(windows[2][:, 0:1536], 0.0)
 
         def group(grouped, g0, j0, j1, copy):
             c = max(c for c in range(len(raw)) if LOADS[c] <= j0)
@@ -128,18 +128,16 @@ def tile_list_hscat_none_kernel(tc, x, w_words, w_scales, wgo, offs, out):
 
         codes_first = tile("codes_first", [P, 256], U32)
         grouped0 = tile("grouped0", [P, 128 * PACK], BF16)
-        group(grouped0, 0, 0, 64, nc.vector.tensor_copy)
-        group(grouped0, 0, 64, 128, nc.scalar.copy)
-        nc.vector.memset(windows[2][:, 888:1280], 0.0)
+        group(grouped0, 0, 0, 128, nc.scalar.copy)
         quantize(0, grouped0, codes_first, 0)
-        nc.vector.memset(windows[2][:, 1272:1664], 0.0)
         multiply(0, 0, 128, codes_first, 0, bank=banks[0][1])
         multiply(1, 0, 128, codes_first, 0, bank=banks[1][1])
         grouped1 = tile("grouped1", [P, 128 * PACK], BF16)
         group(grouped1, 128, 128, 192, nc.vector.tensor_copy)
         group(grouped1, 128, 192, 256, nc.scalar.copy)
-        nc.vector.memset(windows[2][:, 1656:T], 0.0)
+        nc.vector.memset(windows[2][:, 1528:1728], 0.0)
         quantize(1, grouped1, codes_first, 0)
+        nc.vector.memset(windows[2][:, 1720:T], 0.0)
         place(0, 0, 128, slot="raw1", bank=banks[0][1])
         multiply(1, 128, 256, codes_first, 0)
         multiply(2, 0, 256, codes_first, 0)

@@ -19,12 +19,12 @@ PACK = 4
 BLOCKS = M // P
 BANK = 512
 STRIPE = 16
-LOADS = (0, 128, 256, 384, 512, 1024)
-EDGES = (0, 128, 256, 512, 1024)
+EDGES = (0, 128, 384, 512, 1024)
+LOADS = (0, 128, 256, 384, 512, 768, 1024)
 GROUP_COLS = 128
 LINE = 4
 WINDOWS = 3
-STORE_PARTS = (1, 4, 4, 1)
+STORE_PARTS = (2, 4, 2, 1)
 
 
 def tile_list_hscat_none_kernel(tc, x, w_words, w_scales, wgo, offs, out):
@@ -50,26 +50,32 @@ def tile_list_hscat_none_kernel(tc, x, w_words, w_scales, wgo, offs, out):
         def load_x(c):
             nc.sync.dma_start(out=raw[c][:], in_=x_rows[:, :, LOADS[c] : LOADS[c + 1]])
 
+        def load_weights(c0, c1):
+            nc.sync.dma_start(out=out_weights[:, c0:c1], in_=wgo[:, c0:c1])
+
+        def load_scales():
+            for q in range(4):
+                nc.sync.dma_start(
+                    out=w_plane[32 * q : 32 * q + 4, :].bitcast(I32),
+                    in_=w_scales[0, 4 * q : 4 * q + 4, :].bitcast(I32),
+                )
+
         nc.vector.memset(w_plane[:].bitcast(I32), 0)
-        load_x(0)
-        for q in range(4):
-            nc.sync.dma_start(
-                out=w_plane[32 * q : 32 * q + 4, :].bitcast(I32),
-                in_=w_scales[0, 4 * q : 4 * q + 4, :].bitcast(I32),
-            )
-        load_x(1)
-        nc.sync.dma_start(out=words[:, 0:M].bitcast(I32), in_=w_words[0, :, 0:M].bitcast(I32))
-        nc.sync.dma_start(out=out_weights[:, 0:256], in_=wgo[:, 0:256])
         nc.sync.dma_start(offsets[:], offs)
-        nc.sync.dma_start(out=words[:, M : 2 * M].bitcast(I32), in_=w_words[0, :, M : 2 * M].bitcast(I32))
+        load_x(0)
+        load_scales()
+        nc.sync.dma_start(out=words[:].bitcast(I32), in_=w_words[0].bitcast(I32))
+        load_weights(0, 128)
+        load_x(1)
         load_x(2)
         load_x(3)
+        load_weights(128, 512)
         load_x(4)
-        nc.sync.dma_start(out=out_weights[:, 256:1024], in_=wgo[:, 256:1024])
+        load_x(5)
+        load_weights(512, S)
 
-        nc.vector.memset(windows[0][:, 0 : T], 0.0)
-        nc.vector.memset(windows[1][:, 0 : T], 0.0)
-        nc.vector.memset(windows[2][:, 0:1536], 0.0)
+        nc.vector.memset(windows[0][:, 0:2048], 0.0)
+        nc.vector.memset(windows[1][:, 0:2048], 0.0)
 
         def group(grouped, g0, j0, j1, copy):
             c = max(c for c in range(len(raw)) if LOADS[c] <= j0)
@@ -78,42 +84,39 @@ def tile_list_hscat_none_kernel(tc, x, w_words, w_scales, wgo, offs, out):
                 in_=raw[c][:, :, j0 - LOADS[c] : j1 - LOADS[c]].rearrange("p i (r j) -> p r i j", j=LINE),
             )
 
-        def quantize(c, grouped, codes, codes_c0):
-            c0, c1 = EDGES[c], EDGES[c + 1]
-            nc.vector.quantize_mx(
-                out=codes[:, c0 - codes_c0 : c1 - codes_c0].bitcast(FP8X4),
-                scales=x_plane[:, c0:c1],
-                in_=grouped[:],
-            )
-
-        def prepare(c, codes, codes_c0, slot=None):
+        def regroup(c, copy, slot=None):
             c0, c1 = EDGES[c], EDGES[c + 1]
             grouped = tile(f"grouped{c}", [P, (c1 - c0) * PACK], BF16, slot)
             for j in range(c0, c1, GROUP_COLS):
-                group(grouped, c0, j, j + GROUP_COLS, nc.scalar.copy)
-            quantize(c, grouped, codes, codes_c0)
+                group(grouped, c0, j, j + GROUP_COLS, copy)
+            return grouped
 
-        def multiply(b, c0, c1, codes, codes_c0, bank=None):
-            bank = banks[b][c0 // BANK] if bank is None else bank
+        def quantize(c, grouped):
+            c0, c1 = EDGES[c], EDGES[c + 1]
+            codes = tile(f"codes{c}", [P, c1 - c0], U32)
+            nc.vector.quantize_mx(out=codes[:].bitcast(FP8X4), scales=x_plane[:, c0:c1], in_=grouped[:])
+            return codes
+
+        def multiply(b, c, codes):
+            c0, c1 = EDGES[c], EDGES[c + 1]
             nc.tensor.matmul_mx(
-                out=bank[:, c0 % BANK : c0 % BANK + c1 - c0],
+                out=banks[b][c0 // BANK][:, c0 % BANK : c0 % BANK + c1 - c0],
                 lhsT=words[:, 2 * P * b : 2 * P * (b + 1)].bitcast(FP4X4),
                 lhsT_scale=w_plane[:, P * b : P * (b + 1)],
-                rhs=codes[:, c0 - codes_c0 : c1 - codes_c0].bitcast(FP8X4),
+                rhs=codes[:].bitcast(FP8X4),
                 rhs_scale=x_plane[:, c0:c1],
                 start=True,
                 stop=True,
             )
 
-        def place(b, c0, c1, slot=None, bank=None, early=None):
+        def drain(b, c0, c1, slot=None):
             sums = tile(f"sums{b}_{c0}", [P, c1 - c0], F32, slot)
             for h in range(c0 // BANK, (c1 - 1) // BANK + 1):
                 lo, hi = max(c0, BANK * h), min(c1, BANK * (h + 1))
-                source = banks[b][h] if bank is None else bank
-                if early is not None:
-                    nc.scalar.copy(out=sums[:, 0:128], in_=early[:, 0:128])
-                    lo = 128
-                nc.scalar.copy(out=sums[:, lo - c0 : hi - c0], in_=source[:, lo - BANK * h : hi - BANK * h])
+                nc.scalar.copy(out=sums[:, lo - c0 : hi - c0], in_=banks[b][h][:, lo - BANK * h : hi - BANK * h])
+            return sums
+
+        def place(b, c0, c1, sums):
             nc.vector.tensor_tensor(
                 windows[b % WINDOWS][:].indirect(offsets[:, c0 // STRIPE : c1 // STRIPE]),
                 sums[:],
@@ -126,42 +129,36 @@ def tile_list_hscat_none_kernel(tc, x, w_words, w_scales, wgo, offs, out):
             for t in range(0, T, width):
                 nc.sync.dma_start(out=out[P * b : P * (b + 1), t : t + width], in_=windows[b % WINDOWS][:, t : t + width])
 
-        codes_first = tile("codes_first", [P, 256], U32)
-        grouped0 = tile("grouped0", [P, 128 * PACK], BF16)
-        group(grouped0, 0, 0, 128, nc.scalar.copy)
-        quantize(0, grouped0, codes_first, 0)
-        multiply(0, 0, 128, codes_first, 0, bank=banks[0][1])
-        multiply(1, 0, 128, codes_first, 0, bank=banks[1][1])
-        grouped1 = tile("grouped1", [P, 128 * PACK], BF16)
-        group(grouped1, 128, 128, 192, nc.vector.tensor_copy)
-        group(grouped1, 128, 192, 256, nc.scalar.copy)
-        nc.vector.memset(windows[2][:, 1528:1728], 0.0)
-        quantize(1, grouped1, codes_first, 0)
-        nc.vector.memset(windows[2][:, 1720:T], 0.0)
-        place(0, 0, 128, slot="raw1", bank=banks[0][1])
-        multiply(1, 128, 256, codes_first, 0)
-        multiply(2, 0, 256, codes_first, 0)
-        multiply(0, 128, 256, codes_first, 0)
-        multiply(3, 0, 256, codes_first, 0)
-        place(1, 0, 256, early=banks[1][1])
-
-        codes_second = tile("codes_second", [P, 256], U32)
-        prepare(2, codes_second, 256, slot="codes_first")
-        place(2, 0, 256, slot="raw3")
+        grouped = regroup(0, nc.vector.tensor_copy)
+        nc.vector.memset(windows[2][:, 0:512], 0.0)
+        codes = quantize(0, grouped)
+        nc.vector.memset(windows[2][:, 512:2048], 0.0)
         for b in range(BLOCKS):
-            multiply(b, 256, 512, codes_second, 256)
-        place(0, 128, 512)
+            multiply(b, 0, codes)
+        place(0, 0, 128, drain(0, 0, 128))
+        place(1, 0, 128, drain(1, 0, 128))
 
-        codes_third = tile("codes_third", [P, 512], U32)
-        prepare(3, codes_third, 512, slot="codes_second")
-        place(1, 256, 512, slot="raw4")
+        grouped = regroup(1, nc.scalar.copy, slot="codes0")
+        codes = quantize(1, grouped)
+        place(2, 0, 128, drain(2, 0, 128, slot="raw1"))
         for b in range(BLOCKS):
-            multiply(b, 512, S, codes_third, 512)
-        place(0, 512, S)
+            multiply(b, 1, codes)
+
+        codes = quantize(2, regroup(2, nc.scalar.copy))
+        place(0, 128, 384, drain(0, 128, 384))
+        for b in (1, 2, 3, 0):
+            multiply(b, 2, codes)
+        place(1, 128, 512, drain(1, 128, 512))
+
+        codes = quantize(3, regroup(3, nc.scalar.copy, slot="codes1"))
+        place(2, 128, 512, drain(2, 128, 512, slot="raw5"))
+        for b in range(BLOCKS):
+            multiply(b, 3, codes)
+        place(0, 384, S, drain(0, 384, S))
         store(0)
-        place(1, 512, S)
+        place(1, 512, S, drain(1, 512, S))
         store(1)
-        place(2, 256, S, slot="codes_second")
+        place(2, 512, S, drain(2, 512, S))
         store(2)
-        place(3, 0, S, slot="sums1_512")
+        place(3, 0, S, drain(3, 0, S, slot="sums1_512"))
         store(3)

@@ -20,11 +20,18 @@ BLOCKS = M // P
 BANK = 512
 STRIPE = 16
 EDGES = (0, 128, 384, 512, 1024)
-LOADS = (0, 128, 256, 384, 512, 768, 1024)
+LOADS = (0, 128, 384, 512, 768, 1024)
+SHARED = {
+    "codes0": 0,
+    "sums1_0": 0,
+    "sums2_0": 512,
+    "grouped2": 1024,
+    "grouped1": 4032,
+}
 GROUP_COLS = 128
 LINE = 4
 WINDOWS = 3
-STORE_PARTS = (2, 4, 2, 1)
+STORE_PARTS = (1, 4, 4, 1)
 
 
 def tile_list_hscat_none_kernel(tc, x, w_words, w_scales, wgo, offs, out):
@@ -33,9 +40,12 @@ def tile_list_hscat_none_kernel(tc, x, w_words, w_scales, wgo, offs, out):
 
     with ExitStack() as ctx:
         keep = ctx.enter_context(tc.tile_pool(name="keep", bufs=1))
+        reuse = ctx.enter_context(tc.tile_pool(name="reuse", bufs=1))
         psum = ctx.enter_context(tc.psum_pool(name="psum", bufs=1))
 
         def tile(name, shape, dtype, slot=None):
+            if name in SHARED:
+                return reuse.tile(shape, dtype, name=name, offset=SHARED[name], align_bytes=64)
             return keep.tile(shape, dtype, name=name, tag=slot or name, align_bytes=64)
 
         offsets = keep.tile([P, S // STRIPE], U16, name="offsets")
@@ -65,13 +75,12 @@ def tile_list_hscat_none_kernel(tc, x, w_words, w_scales, wgo, offs, out):
         load_x(0)
         load_scales()
         nc.sync.dma_start(out=words[:].bitcast(I32), in_=w_words[0].bitcast(I32))
-        load_weights(0, 128)
         load_x(1)
+        load_weights(0, 128)
         load_x(2)
-        load_x(3)
         load_weights(128, 512)
+        load_x(3)
         load_x(4)
-        load_x(5)
         load_weights(512, S)
 
         nc.vector.memset(windows[0][:, 0:2048], 0.0)
@@ -93,8 +102,8 @@ def tile_list_hscat_none_kernel(tc, x, w_words, w_scales, wgo, offs, out):
 
         def quantize(c, grouped):
             c0, c1 = EDGES[c], EDGES[c + 1]
-            codes = tile(f"codes{c}", [P, c1 - c0], U32)
-            nc.vector.quantize_mx(out=codes[:].bitcast(FP8X4), scales=x_plane[:, c0:c1], in_=grouped[:])
+            codes = tile(f"codes{c}", [P, S if c == 0 else c1 - c0], U32)[:, 0 : c1 - c0]
+            nc.vector.quantize_mx(out=codes.bitcast(FP8X4), scales=x_plane[:, c0:c1], in_=grouped[:])
             return codes
 
         def multiply(b, c, codes):
@@ -103,7 +112,7 @@ def tile_list_hscat_none_kernel(tc, x, w_words, w_scales, wgo, offs, out):
                 out=banks[b][c0 // BANK][:, c0 % BANK : c0 % BANK + c1 - c0],
                 lhsT=words[:, 2 * P * b : 2 * P * (b + 1)].bitcast(FP4X4),
                 lhsT_scale=w_plane[:, P * b : P * (b + 1)],
-                rhs=codes[:].bitcast(FP8X4),
+                rhs=codes.bitcast(FP8X4),
                 rhs_scale=x_plane[:, c0:c1],
                 start=True,
                 stop=True,
@@ -135,12 +144,13 @@ def tile_list_hscat_none_kernel(tc, x, w_words, w_scales, wgo, offs, out):
         nc.vector.memset(windows[2][:, 512:2048], 0.0)
         for b in range(BLOCKS):
             multiply(b, 0, codes)
+        grouped = tile("grouped1", [P, 256 * PACK], BF16)
+        group(grouped, 128, 128, 256, nc.vector.tensor_copy)
         place(0, 0, 128, drain(0, 0, 128))
-        place(1, 0, 128, drain(1, 0, 128))
-
-        grouped = regroup(1, nc.scalar.copy, slot="codes0")
+        group(grouped, 128, 256, 384, nc.scalar.copy)
         codes = quantize(1, grouped)
-        place(2, 0, 128, drain(2, 0, 128, slot="raw1"))
+        place(1, 0, 128, drain(1, 0, 128))
+        place(2, 0, 128, drain(2, 0, 128))
         for b in range(BLOCKS):
             multiply(b, 1, codes)
 
@@ -151,7 +161,7 @@ def tile_list_hscat_none_kernel(tc, x, w_words, w_scales, wgo, offs, out):
         place(1, 128, 512, drain(1, 128, 512))
 
         codes = quantize(3, regroup(3, nc.scalar.copy, slot="codes1"))
-        place(2, 128, 512, drain(2, 128, 512, slot="raw5"))
+        place(2, 128, 512, drain(2, 128, 512, slot="raw4"))
         for b in range(BLOCKS):
             multiply(b, 3, codes)
         place(0, 384, S, drain(0, 384, S))

@@ -23,10 +23,10 @@ EDGES = (0, 128, 384, 512, 1024)
 LOADS = (0, 128, 384, 512, 768, 1024)
 SHARED = {
     "codes0": 0,
-    "sums1_0": 0,
-    "sums2_0": 512,
-    "grouped2": 1024,
-    "grouped1": 4032,
+    "grouped1_late": 0,
+    "sums1_0": 1024,
+    "sums2_0": 1536,
+    "grouped2": 2048,
 }
 GROUP_COLS = 128
 LINE = 4
@@ -71,11 +71,11 @@ def tile_list_hscat_none_kernel(tc, x, w_words, w_scales, wgo, offs, out):
                 )
 
         nc.vector.memset(w_plane[:].bitcast(I32), 0)
-        nc.sync.dma_start(offsets[:], offs)
         load_x(0)
-        load_scales()
         nc.sync.dma_start(out=words[:].bitcast(I32), in_=w_words[0].bitcast(I32))
+        load_scales()
         load_x(1)
+        nc.sync.dma_start(offsets[:], offs)
         load_weights(0, 128)
         load_x(2)
         load_weights(128, 512)
@@ -144,11 +144,14 @@ def tile_list_hscat_none_kernel(tc, x, w_words, w_scales, wgo, offs, out):
         nc.vector.memset(windows[2][:, 512:2048], 0.0)
         for b in range(BLOCKS):
             multiply(b, 0, codes)
-        grouped = tile("grouped1", [P, 256 * PACK], BF16)
-        group(grouped, 128, 128, 256, nc.vector.tensor_copy)
+        early = tile("grouped1_early", [P, 128 * PACK], BF16)
+        group(early, 128, 128, 256, nc.vector.tensor_copy)
         place(0, 0, 128, drain(0, 0, 128))
-        group(grouped, 128, 256, 384, nc.scalar.copy)
-        codes = quantize(1, grouped)
+        late = tile("grouped1_late", [P, 128 * PACK], BF16)
+        group(late, 256, 256, 384, nc.scalar.copy)
+        codes = tile("codes1", [P, 256], U32, slot="raw1")[:]
+        nc.vector.quantize_mx(out=codes[:, 0:128].bitcast(FP8X4), scales=x_plane[:, 128:256], in_=early[:])
+        nc.vector.quantize_mx(out=codes[:, 128:256].bitcast(FP8X4), scales=x_plane[:, 256:384], in_=late[:])
         place(1, 0, 128, drain(1, 0, 128))
         place(2, 0, 128, drain(2, 0, 128))
         for b in range(BLOCKS):
@@ -160,7 +163,7 @@ def tile_list_hscat_none_kernel(tc, x, w_words, w_scales, wgo, offs, out):
             multiply(b, 2, codes)
         place(1, 128, 512, drain(1, 128, 512))
 
-        codes = quantize(3, regroup(3, nc.scalar.copy, slot="codes1"))
+        codes = quantize(3, regroup(3, nc.scalar.copy, slot="raw1"))
         place(2, 128, 512, drain(2, 128, 512, slot="raw4"))
         for b in range(BLOCKS):
             multiply(b, 3, codes)

@@ -19,18 +19,14 @@ PACK = 4
 BLOCKS = M // P
 BANK = 512
 STRIPE = 16
-EDGES = (0, 128, 384, 512, 1024)
-LOADS = (0, 128, 384, 512, 768, 1024)
-SHARED = {
-    "codes0": 0,
-    "grouped1_late": 0,
-    "sums1_0": 1024,
-    "sums2_0": 1536,
-    "grouped2": 2048,
-}
-GROUP_COLS = 128
+QUADRANT = 32
 LINE = 4
 WINDOWS = 3
+CHUNKS = (0, 128, 384, 512, 1024)
+LOADS = (0, 128, 384, 512, 768, 1024)
+GROUP_COLS = 128
+VECTOR_SHARE = 96
+CLEAR_EARLY = 512
 STORE_PARTS = (1, 4, 4, 1)
 
 
@@ -40,13 +36,10 @@ def tile_list_hscat_none_kernel(tc, x, w_words, w_scales, wgo, offs, out):
 
     with ExitStack() as ctx:
         keep = ctx.enter_context(tc.tile_pool(name="keep", bufs=1))
-        reuse = ctx.enter_context(tc.tile_pool(name="reuse", bufs=1))
         psum = ctx.enter_context(tc.psum_pool(name="psum", bufs=1))
 
-        def tile(name, shape, dtype, slot=None):
-            if name in SHARED:
-                return reuse.tile(shape, dtype, name=name, offset=SHARED[name], align_bytes=64)
-            return keep.tile(shape, dtype, name=name, tag=slot or name, align_bytes=64)
+        def tile(name, shape, dtype, on=None):
+            return keep.tile(shape, dtype, name=name, tag=on or name, align_bytes=64)
 
         offsets = keep.tile([P, S // STRIPE], U16, name="offsets")
         words = tile("words", [P, 2 * M], U8)
@@ -54,82 +47,61 @@ def tile_list_hscat_none_kernel(tc, x, w_words, w_scales, wgo, offs, out):
         out_weights = tile("out_weights", [P, S], F32)
         raw = [tile(f"raw{c}", [P, PACK, LOADS[c + 1] - LOADS[c]], F32) for c in range(len(LOADS) - 1)]
         x_plane = tile("x_plane", [P, S], U8)
-        banks = [[psum.tile([P, BANK], F32, name=f"bank{b}{h}") for h in range(2)] for b in range(BLOCKS)]
+        banks = [[psum.tile([P, BANK], F32, name=f"bank{b}{h}") for h in range(S // BANK)] for b in range(BLOCKS)]
         windows = [tile(f"window{b}", [P, T], F32) for b in range(WINDOWS)]
 
         def load_x(c):
             nc.sync.dma_start(out=raw[c][:], in_=x_rows[:, :, LOADS[c] : LOADS[c + 1]])
 
-        def load_weights(c0, c1):
-            nc.sync.dma_start(out=out_weights[:, c0:c1], in_=wgo[:, c0:c1])
+        def load_weights(j0, j1):
+            nc.sync.dma_start(out=out_weights[:, j0:j1], in_=wgo[:, j0:j1])
 
-        def load_scales():
-            for q in range(4):
-                nc.sync.dma_start(
-                    out=w_plane[32 * q : 32 * q + 4, :].bitcast(I32),
-                    in_=w_scales[0, 4 * q : 4 * q + 4, :].bitcast(I32),
-                )
-
-        nc.vector.memset(w_plane[:].bitcast(I32), 0)
-        load_x(0)
-        nc.sync.dma_start(out=words[:].bitcast(I32), in_=w_words[0].bitcast(I32))
-        load_scales()
-        load_x(1)
-        nc.sync.dma_start(offsets[:], offs)
-        load_weights(0, 128)
-        load_x(2)
-        load_weights(128, 512)
-        load_x(3)
-        load_x(4)
-        load_weights(512, S)
-
-        nc.vector.memset(windows[0][:, 0:2048], 0.0)
-        nc.vector.memset(windows[1][:, 0:2048], 0.0)
-
-        def group(grouped, g0, j0, j1, copy):
-            c = max(c for c in range(len(raw)) if LOADS[c] <= j0)
+        def group(grouped, c, j0, j1, copy):
+            load = max(n for n in range(len(raw)) if LOADS[n] <= j0)
+            into = grouped[:, PACK * (j0 - CHUNKS[c]) : PACK * (j1 - CHUNKS[c])]
+            source = raw[load][:, :, j0 - LOADS[load] : j1 - LOADS[load]]
             copy(
-                out=grouped[:, PACK * (j0 - g0) : PACK * (j1 - g0)].rearrange("p (r j i) -> p r i j", j=LINE, i=PACK),
-                in_=raw[c][:, :, j0 - LOADS[c] : j1 - LOADS[c]].rearrange("p i (r j) -> p r i j", j=LINE),
+                out=into.rearrange("p (r j i) -> p r i j", j=LINE, i=PACK),
+                in_=source.rearrange("p i (r j) -> p r i j", j=LINE),
             )
 
-        def regroup(c, copy, slot=None):
-            c0, c1 = EDGES[c], EDGES[c + 1]
-            grouped = tile(f"grouped{c}", [P, (c1 - c0) * PACK], BF16, slot)
-            for j in range(c0, c1, GROUP_COLS):
-                group(grouped, c0, j, j + GROUP_COLS, copy)
+        def grouped_tile(c, on=None):
+            return tile(f"grouped{c}", [P, (CHUNKS[c + 1] - CHUNKS[c]) * PACK], BF16, on)
+
+        def group_chunk(c, copy, on=None):
+            grouped = grouped_tile(c, on)
+            for j in range(CHUNKS[c], CHUNKS[c + 1], GROUP_COLS):
+                group(grouped, c, j, j + GROUP_COLS, copy)
             return grouped
 
         def quantize(c, grouped):
-            c0, c1 = EDGES[c], EDGES[c + 1]
-            codes = tile(f"codes{c}", [P, S if c == 0 else c1 - c0], U32)[:, 0 : c1 - c0]
-            nc.vector.quantize_mx(out=codes.bitcast(FP8X4), scales=x_plane[:, c0:c1], in_=grouped[:])
+            j0, j1 = CHUNKS[c], CHUNKS[c + 1]
+            codes = tile(f"codes{c}", [P, j1 - j0], U32)
+            nc.vector.quantize_mx(out=codes[:].bitcast(FP8X4), scales=x_plane[:, j0:j1], in_=grouped[:])
             return codes
 
-        def multiply(b, c, codes):
-            c0, c1 = EDGES[c], EDGES[c + 1]
-            nc.tensor.matmul_mx(
-                out=banks[b][c0 // BANK][:, c0 % BANK : c0 % BANK + c1 - c0],
-                lhsT=words[:, 2 * P * b : 2 * P * (b + 1)].bitcast(FP4X4),
-                lhsT_scale=w_plane[:, P * b : P * (b + 1)],
-                rhs=codes.bitcast(FP8X4),
-                rhs_scale=x_plane[:, c0:c1],
-                start=True,
-                stop=True,
-            )
+        def multiply(c, codes, blocks):
+            j0, j1 = CHUNKS[c], CHUNKS[c + 1]
+            for b in blocks:
+                nc.tensor.matmul_mx(
+                    out=banks[b][j0 // BANK][:, j0 % BANK : j0 % BANK + j1 - j0],
+                    lhsT=words[:, 2 * P * b : 2 * P * (b + 1)].bitcast(FP4X4),
+                    lhsT_scale=w_plane[:, P * b : P * (b + 1)],
+                    rhs=codes[:].bitcast(FP8X4),
+                    rhs_scale=x_plane[:, j0:j1],
+                    start=True,
+                    stop=True,
+                )
 
-        def drain(b, c0, c1, slot=None):
-            sums = tile(f"sums{b}_{c0}", [P, c1 - c0], F32, slot)
-            for h in range(c0 // BANK, (c1 - 1) // BANK + 1):
-                lo, hi = max(c0, BANK * h), min(c1, BANK * (h + 1))
-                nc.scalar.copy(out=sums[:, lo - c0 : hi - c0], in_=banks[b][h][:, lo - BANK * h : hi - BANK * h])
-            return sums
-
-        def place(b, c0, c1, sums):
+        def place(b, j0, j1, on=None):
+            sums = tile(f"sums{b}_{j0}", [P, j1 - j0], F32, on)
+            for h in range(j0 // BANK, (j1 - 1) // BANK + 1):
+                lo, hi = max(j0, BANK * h), min(j1, BANK * (h + 1))
+                nc.scalar.copy(out=sums[:, lo - j0 : hi - j0], in_=banks[b][h][:, lo - BANK * h : hi - BANK * h])
             nc.vector.tensor_tensor(
-                windows[b % WINDOWS][:].indirect(offsets[:, c0 // STRIPE : c1 // STRIPE]),
+                windows[b % WINDOWS][:].indirect(offsets[:, j0 // STRIPE : j1 // STRIPE]),
                 sums[:],
-                out_weights[:, c0:c1],
+                out_weights[:, j0:j1],
                 mybir.AluOpType.mult,
             )
 
@@ -138,40 +110,55 @@ def tile_list_hscat_none_kernel(tc, x, w_words, w_scales, wgo, offs, out):
             for t in range(0, T, width):
                 nc.sync.dma_start(out=out[P * b : P * (b + 1), t : t + width], in_=windows[b % WINDOWS][:, t : t + width])
 
-        grouped = regroup(0, nc.vector.tensor_copy)
-        nc.vector.memset(windows[2][:, 0:512], 0.0)
+        start0, start1, start2, start3, end = CHUNKS
+
+        nc.vector.memset(w_plane[:].bitcast(I32), 0)
+        load_x(0)
+        nc.sync.dma_start(out=words[:].bitcast(I32), in_=w_words[0].bitcast(I32))
+        for q in range(P // QUADRANT):
+            nc.sync.dma_start(
+                out=w_plane[QUADRANT * q : QUADRANT * q + 4, :].bitcast(I32),
+                in_=w_scales[0, 4 * q : 4 * q + 4, :].bitcast(I32),
+            )
+        load_x(1)
+        nc.sync.dma_start(offsets[:], offs)
+        load_weights(start0, start1)
+        load_x(2)
+        load_weights(start1, start3)
+        load_x(3)
+        load_x(4)
+        load_weights(start3, end)
+
+        nc.vector.memset(windows[0][:], 0.0)
+        nc.vector.memset(windows[1][:], 0.0)
+
+        grouped = group_chunk(0, nc.vector.tensor_copy)
+        nc.vector.memset(windows[2][:, 0:CLEAR_EARLY], 0.0)
         codes = quantize(0, grouped)
-        nc.vector.memset(windows[2][:, 512:2048], 0.0)
-        for b in range(BLOCKS):
-            multiply(b, 0, codes)
-        early = tile("grouped1_early", [P, 128 * PACK], BF16)
-        group(early, 128, 128, 256, nc.vector.tensor_copy)
-        place(0, 0, 128, drain(0, 0, 128))
-        late = tile("grouped1_late", [P, 128 * PACK], BF16)
-        group(late, 256, 256, 384, nc.scalar.copy)
-        codes = tile("codes1", [P, 256], U32, slot="raw1")[:]
-        nc.vector.quantize_mx(out=codes[:, 0:128].bitcast(FP8X4), scales=x_plane[:, 128:256], in_=early[:])
-        nc.vector.quantize_mx(out=codes[:, 128:256].bitcast(FP8X4), scales=x_plane[:, 256:384], in_=late[:])
-        place(1, 0, 128, drain(1, 0, 128))
-        place(2, 0, 128, drain(2, 0, 128))
-        for b in range(BLOCKS):
-            multiply(b, 1, codes)
+        nc.vector.memset(windows[2][:, CLEAR_EARLY:T], 0.0)
+        multiply(0, codes, range(BLOCKS))
 
-        codes = quantize(2, regroup(2, nc.scalar.copy))
-        place(0, 128, 384, drain(0, 128, 384))
-        for b in (1, 2, 3, 0):
-            multiply(b, 2, codes)
-        place(1, 128, 512, drain(1, 128, 512))
+        grouped = grouped_tile(1)
+        group(grouped, 1, start1, start1 + VECTOR_SHARE, nc.vector.tensor_copy)
+        place(0, start0, start1)
+        group(grouped, 1, start1 + VECTOR_SHARE, start2, nc.scalar.copy)
+        codes = quantize(1, grouped)
+        place(1, start0, start1)
+        place(2, start0, start1)
+        multiply(1, codes, range(BLOCKS))
 
-        codes = quantize(3, regroup(3, nc.scalar.copy, slot="raw1"))
-        place(2, 128, 512, drain(2, 128, 512, slot="raw4"))
-        for b in range(BLOCKS):
-            multiply(b, 3, codes)
-        place(0, 384, S, drain(0, 384, S))
+        codes = quantize(2, group_chunk(2, nc.scalar.copy))
+        place(0, start1, start2)
+        multiply(2, codes, (1, 2, 3, 0))
+        place(1, start1, start3)
+
+        codes = quantize(3, group_chunk(3, nc.scalar.copy, on="codes1"))
+        place(2, start1, start3, on="raw4")
+        multiply(3, codes, range(BLOCKS))
+        place(0, start2, end)
         store(0)
-        place(1, 512, S, drain(1, 512, S))
-        store(1)
-        place(2, 512, S, drain(2, 512, S))
-        store(2)
-        place(3, 0, S, drain(3, 0, S, slot="sums1_512"))
+        for b in (1, 2):
+            place(b, start3, end)
+            store(b)
+        place(3, start0, end, on=f"sums1_{start3}")
         store(3)

@@ -26,8 +26,8 @@ CHUNKS = (0, 128, 384, 512, 1024)
 LOADS = (0, 128, 384, 512, 768, 1024)
 GROUP_COLS = 128
 VECTOR_SHARE = 96
-CLEAR_EARLY = 512
-STORE_PARTS = (1, 4, 4, 1)
+CLEAR_EARLY = 384
+STORE_PARTS = (2, 2, 4, 1)
 
 
 def tile_list_hscat_none_kernel(tc, x, w_words, w_scales, wgo, offs, out):
@@ -36,22 +36,29 @@ def tile_list_hscat_none_kernel(tc, x, w_words, w_scales, wgo, offs, out):
 
     with ExitStack() as ctx:
         keep = ctx.enter_context(tc.tile_pool(name="keep", bufs=1))
+        second = ctx.enter_context(tc.tile_pool(name="second", bufs=1))
         psum = ctx.enter_context(tc.psum_pool(name="psum", bufs=1))
 
         def tile(name, shape, dtype, on=None):
+            if isinstance(on, int):
+                return second.tile(shape, dtype, name=name, offset=on, align_bytes=64)
             return keep.tile(shape, dtype, name=name, tag=on or name, align_bytes=64)
 
         offsets = keep.tile([P, S // STRIPE], U16, name="offsets")
-        words = tile("words", [P, 2 * M], U8)
+        words = [tile(f"words{h}", [P, M], U8) for h in range(2)]
         w_plane = tile("w_plane", [P, M], U8)
         out_weights = tile("out_weights", [P, S], F32)
-        raw = [tile(f"raw{c}", [P, PACK, LOADS[c + 1] - LOADS[c]], F32) for c in range(len(LOADS) - 1)]
+        raw = [tile(f"raw{c}", [P, PACK, LOADS[c + 1] - LOADS[c]], F32, 0 if c == 1 else None) for c in range(len(LOADS) - 1)]
         x_plane = tile("x_plane", [P, S], U8)
-        banks = [[psum.tile([P, BANK], F32, name=f"bank{b}{h}") for h in range(S // BANK)] for b in range(BLOCKS)]
+        codes = tile("codes", [P, S], U32)
+        banks = [psum.tile([P, BANK], F32, name=f"bank{n}") for n in range(8)]
         windows = [tile(f"window{b}", [P, T], F32) for b in range(WINDOWS)]
 
         def load_x(c):
             nc.sync.dma_start(out=raw[c][:], in_=x_rows[:, :, LOADS[c] : LOADS[c + 1]])
+
+        def load_words(h):
+            nc.sync.dma_start(out=words[h][:].bitcast(I32), in_=w_words[0, :, M * h : M * (h + 1)].bitcast(I32))
 
         def load_weights(j0, j1):
             nc.sync.dma_start(out=out_weights[:, j0:j1], in_=wgo[:, j0:j1])
@@ -76,28 +83,26 @@ def tile_list_hscat_none_kernel(tc, x, w_words, w_scales, wgo, offs, out):
 
         def quantize(c, grouped):
             j0, j1 = CHUNKS[c], CHUNKS[c + 1]
-            codes = tile(f"codes{c}", [P, j1 - j0], U32)
-            nc.vector.quantize_mx(out=codes[:].bitcast(FP8X4), scales=x_plane[:, j0:j1], in_=grouped[:])
-            return codes
+            nc.vector.quantize_mx(out=codes[:, j0:j1].bitcast(FP8X4), scales=x_plane[:, j0:j1], in_=grouped[:])
 
-        def multiply(c, codes, blocks):
-            j0, j1 = CHUNKS[c], CHUNKS[c + 1]
-            for b in blocks:
-                nc.tensor.matmul_mx(
-                    out=banks[b][j0 // BANK][:, j0 % BANK : j0 % BANK + j1 - j0],
-                    lhsT=words[:, 2 * P * b : 2 * P * (b + 1)].bitcast(FP4X4),
-                    lhsT_scale=w_plane[:, P * b : P * (b + 1)],
-                    rhs=codes[:].bitcast(FP8X4),
-                    rhs_scale=x_plane[:, j0:j1],
-                    start=True,
-                    stop=True,
-                )
+        def multiply(b, j0, j1, bank, at=0):
+            nc.tensor.matmul_mx(
+                out=banks[bank][:, at : at + j1 - j0],
+                lhsT=words[b // 2][:, 2 * P * (b % 2) : 2 * P * (b % 2 + 1)].bitcast(FP4X4),
+                lhsT_scale=w_plane[:, P * b : P * (b + 1)],
+                rhs=codes[:, j0:j1].bitcast(FP8X4),
+                rhs_scale=x_plane[:, j0:j1],
+                start=True,
+                stop=True,
+            )
 
-        def place(b, j0, j1, on=None):
-            sums = tile(f"sums{b}_{j0}", [P, j1 - j0], F32, on)
-            for h in range(j0 // BANK, (j1 - 1) // BANK + 1):
-                lo, hi = max(j0, BANK * h), min(j1, BANK * (h + 1))
-                nc.scalar.copy(out=sums[:, lo - j0 : hi - j0], in_=banks[b][h][:, lo - BANK * h : hi - BANK * h])
+        def sums_tile(b, j0, j1, on=None):
+            return tile(f"sums{b}_{j0}", [P, j1 - j0], F32, on)
+
+        def fetch(into, bank, copy=nc.scalar.copy):
+            copy(out=into, in_=banks[bank][:, 0 : into.shape[1]])
+
+        def scatter(b, j0, j1, sums):
             nc.vector.tensor_tensor(
                 windows[b % WINDOWS][:].indirect(offsets[:, j0 // STRIPE : j1 // STRIPE]),
                 sums[:],
@@ -114,7 +119,7 @@ def tile_list_hscat_none_kernel(tc, x, w_words, w_scales, wgo, offs, out):
 
         nc.vector.memset(w_plane[:].bitcast(I32), 0)
         load_x(0)
-        nc.sync.dma_start(out=words[:].bitcast(I32), in_=w_words[0].bitcast(I32))
+        load_words(0)
         for q in range(P // QUADRANT):
             nc.sync.dma_start(
                 out=w_plane[QUADRANT * q : QUADRANT * q + 4, :].bitcast(I32),
@@ -123,6 +128,7 @@ def tile_list_hscat_none_kernel(tc, x, w_words, w_scales, wgo, offs, out):
         load_x(1)
         nc.sync.dma_start(offsets[:], offs)
         load_weights(start0, start1)
+        load_words(1)
         load_x(2)
         load_weights(start1, start3)
         load_x(3)
@@ -134,31 +140,57 @@ def tile_list_hscat_none_kernel(tc, x, w_words, w_scales, wgo, offs, out):
 
         grouped = group_chunk(0, nc.vector.tensor_copy)
         nc.vector.memset(windows[2][:, 0:CLEAR_EARLY], 0.0)
-        codes = quantize(0, grouped)
+        quantize(0, grouped)
         nc.vector.memset(windows[2][:, CLEAR_EARLY:T], 0.0)
-        multiply(0, codes, range(BLOCKS))
+        for b in range(WINDOWS):
+            multiply(b, start0, start1, b)
 
+        sums = sums_tile(0, start0, start1)
+        fetch(sums[:], 0, nc.vector.tensor_copy)
         grouped = grouped_tile(1)
         group(grouped, 1, start1, start1 + VECTOR_SHARE, nc.vector.tensor_copy)
-        place(0, start0, start1)
+        scatter(0, start0, start1, sums)
         group(grouped, 1, start1 + VECTOR_SHARE, start2, nc.scalar.copy)
-        codes = quantize(1, grouped)
-        place(1, start0, start1)
-        place(2, start0, start1)
-        multiply(1, codes, range(BLOCKS))
-
-        codes = quantize(2, group_chunk(2, nc.scalar.copy))
-        place(0, start1, start2)
-        multiply(2, codes, (1, 2, 3, 0))
-        place(1, start1, start3)
-
-        codes = quantize(3, group_chunk(3, nc.scalar.copy, on="codes1"))
-        place(2, start1, start3, on="raw4")
-        multiply(3, codes, range(BLOCKS))
-        place(0, start2, end)
-        store(0)
+        quantize(1, grouped)
         for b in (1, 2):
-            place(b, start3, end)
+            sums = sums_tile(b, start0, start1, on=4 * start1 * (b - 1))
+            fetch(sums[:], b)
+            scatter(b, start0, start1, sums)
+        multiply(0, start1, start2, 2)
+
+        quantize(2, group_chunk(2, nc.scalar.copy, on=8 * start1))
+        sums = sums_tile(0, start1, start2)
+        fetch(sums[:], 2)
+        scatter(0, start1, start2, sums)
+        multiply(1, start1, start2, 2)
+        multiply(1, start2, start3, 1)
+        multiply(0, start2, start3, 0)
+        multiply(2, 2 * start1, start3, 3, start1)
+        multiply(2, start1, 2 * start1, 3)
+        multiply(3, start0, start3, 4)
+        sums = sums_tile(1, start1, start3)
+        fetch(sums[:, 0 : start2 - start1], 2)
+        fetch(sums[:, start2 - start1 : start3 - start1], 1)
+        scatter(1, start1, start3, sums)
+
+        quantize(3, group_chunk(3, nc.scalar.copy, on="grouped0"))
+        sums = sums_tile(2, start1, start3, on="raw4")
+        fetch(sums[:], 3)
+        scatter(2, start1, start3, sums)
+        for b, bank in enumerate((5, 6, 2, 7)):
+            multiply(b, start3, end, bank)
+        sums = sums_tile(0, start2, end)
+        fetch(sums[:, 0 : start3 - start2], 0)
+        fetch(sums[:, start3 - start2 : end - start2], 5)
+        scatter(0, start2, end, sums)
+        store(0)
+        for b, bank in ((1, 6), (2, 2)):
+            sums = sums_tile(b, start3, end)
+            fetch(sums[:], bank)
+            scatter(b, start3, end, sums)
             store(b)
-        place(3, start0, end, on=f"sums1_{start3}")
+        sums = sums_tile(3, start0, end, on=f"sums1_{start3}")
+        fetch(sums[:, 0:BANK], 4)
+        fetch(sums[:, BANK:S], 7)
+        scatter(3, start0, end, sums)
         store(3)

@@ -99,8 +99,8 @@ def tile_list_hscat_none_kernel(tc, x, w_words, w_scales, wgo, offs, out):
         def sums_tile(b, j0, j1, on=None):
             return tile(f"sums{b}_{j0}", [P, j1 - j0], F32, on)
 
-        def fetch(into, bank, copy=nc.scalar.copy):
-            copy(out=into, in_=banks[bank][:, 0 : into.shape[1]])
+        def fetch(into, bank):
+            nc.scalar.copy(out=into, in_=banks[bank][:, 0 : into.shape[1]])
 
         def scatter(b, j0, j1, sums):
             nc.vector.tensor_tensor(
@@ -146,7 +146,7 @@ def tile_list_hscat_none_kernel(tc, x, w_words, w_scales, wgo, offs, out):
             multiply(b, start0, start1, b)
 
         sums = sums_tile(0, start0, start1)
-        fetch(sums[:], 0, nc.vector.tensor_copy)
+        fetch(sums[:], 0)
         grouped = grouped_tile(1)
         group(grouped, 1, start1, start1 + VECTOR_SHARE, nc.vector.tensor_copy)
         scatter(0, start0, start1, sums)

@@ -21,6 +21,7 @@ BANK = 512
 STRIPE = 16
 QUADRANT = 32
 LINE = 4
+ALIGN = 512
 WINDOWS = 3
 CHUNKS = (0, 128, 384, 512, 1024)
 LOADS = (0, 128, 384, 512, 768, 1024)
@@ -41,8 +42,8 @@ def tile_list_hscat_none_kernel(tc, x, w_words, w_scales, wgo, offs, out):
 
         def tile(name, shape, dtype, on=None):
             if isinstance(on, int):
-                return second.tile(shape, dtype, name=name, offset=on, align_bytes=64)
-            return keep.tile(shape, dtype, name=name, tag=on or name, align_bytes=64)
+                return second.tile(shape, dtype, name=name, offset=on, align_bytes=ALIGN)
+            return keep.tile(shape, dtype, name=name, tag=on or name, align_bytes=ALIGN)
 
         offsets = keep.tile([P, S // STRIPE], U16, name="offsets")
         words = [tile(f"words{h}", [P, M], U8) for h in range(2)]

from contextlib import ExitStack

import concourse.mybir as mybir

K, M, T, S = 512, 512, 2048, 1024
FLOPS = 2 * K * M * S

F32 = mybir.dt.float32
BF16 = mybir.dt.bfloat16
I32 = mybir.dt.int32
U32 = mybir.dt.uint32
U16 = mybir.dt.uint16
U8 = mybir.dt.uint8
FP8X4 = mybir.dt.float8_e4m3fn_x4
FP4X4 = mybir.dt.float4_e2m1fn_x4

P = 128
PACK = 4
BLOCKS = M // P
BANK = 512
STRIPE = 16
QUADRANT = 32
LINE = 4
ALIGN = 512
WINDOWS = 3
CHUNKS = (0, 128, 384, 512, 1024)
LOADS = (0, 128, 384, 512, 768, 1024)
GROUP_COLS = 128
VECTOR_SHARE = 96
CLEAR_EARLY = 384
STORE_PARTS = (2, 2, 4, 1)


def tile_list_hscat_none_kernel(tc, x, w_words, w_scales, wgo, offs, out):
    nc = tc.nc
    x_rows = x.rearrange("(p i) j -> p i j", i=PACK)

    with ExitStack() as ctx:
        keep = ctx.enter_context(tc.tile_pool(name="keep", bufs=1))
        second = ctx.enter_context(tc.tile_pool(name="second", bufs=1))
        psum = ctx.enter_context(tc.psum_pool(name="psum", bufs=1))

        def tile(name, shape, dtype, on=None):
            if isinstance(on, int):
                return second.tile(shape, dtype, name=name, offset=on, align_bytes=ALIGN)
            return keep.tile(shape, dtype, name=name, tag=on or name, align_bytes=ALIGN)

        offsets = keep.tile([P, S // STRIPE], U16, name="offsets")
        words = [tile(f"words{h}", [P, M], U8) for h in range(2)]
        w_plane = tile("w_plane", [P, M], U8)
        out_weights = tile("out_weights", [P, S], F32)
        raw = [tile(f"raw{c}", [P, PACK, LOADS[c + 1] - LOADS[c]], F32, 0 if c == 1 else None) for c in range(len(LOADS) - 1)]
        x_plane = tile("x_plane", [P, S], U8)
        codes = tile("codes", [P, S], U32)
        banks = [psum.tile([P, BANK], F32, name=f"bank{n}") for n in range(8)]
        windows = [tile(f"window{b}", [P, T], F32) for b in range(WINDOWS)]

        def load_x(c):
            nc.sync.dma_start(out=raw[c][:], in_=x_rows[:, :, LOADS[c] : LOADS[c + 1]])

        def load_words(h):
            nc.sync.dma_start(out=words[h][:].bitcast(I32), in_=w_words[0, :, M * h : M * (h + 1)].bitcast(I32))

        def load_weights(j0, j1):
            nc.sync.dma_start(out=out_weights[:, j0:j1], in_=wgo[:, j0:j1])

        def group(grouped, c, j0, j1, copy):
            load = max(n for n in range(len(raw)) if LOADS[n] <= j0)
            into = grouped[:, PACK * (j0 - CHUNKS[c]) : PACK * (j1 - CHUNKS[c])]
            source = raw[load][:, :, j0 - LOADS[load] : j1 - LOADS[load]]
            copy(
                out=into.rearrange("p (r j i) -> p r i j", j=LINE, i=PACK),
                in_=source.rearrange("p i (r j) -> p r i j", j=LINE),
            )

        def grouped_tile(c, on=None):
            return tile(f"grouped{c}", [P, (CHUNKS[c + 1] - CHUNKS[c]) * PACK], BF16, on)

        def group_chunk(c, copy, on=None):
            grouped = grouped_tile(c, on)
            for j in range(CHUNKS[c], CHUNKS[c + 1], GROUP_COLS):
                group(grouped, c, j, j + GROUP_COLS, copy)
            return grouped

        def quantize(c, grouped):
            j0, j1 = CHUNKS[c], CHUNKS[c + 1]
            nc.vector.quantize_mx(out=codes[:, j0:j1].bitcast(FP8X4), scales=x_plane[:, j0:j1], in_=grouped[:])

        def multiply(b, j0, j1, bank, at=0):
            nc.tensor.matmul_mx(
                out=banks[bank][:, at : at + j1 - j0],
                lhsT=words[b // 2][:, 2 * P * (b % 2) : 2 * P * (b % 2 + 1)].bitcast(FP4X4),
                lhsT_scale=w_plane[:, P * b : P * (b + 1)],
                rhs=codes[:, j0:j1].bitcast(FP8X4),
                rhs_scale=x_plane[:, j0:j1],
                start=True,
                stop=True,
            )

        def sums_tile(b, j0, j1, on=None):
            return tile(f"sums{b}_{j0}", [P, j1 - j0], F32, on)

        def fetch(into, bank):
            nc.scalar.copy(out=into, in_=banks[bank][:, 0 : into.shape[1]])

        def scatter(b, j0, j1, sums):
            nc.vector.tensor_tensor(
                windows[b % WINDOWS][:].indirect(offsets[:, j0 // STRIPE : j1 // STRIPE]),
                sums[:],
                out_weights[:, j0:j1],
                mybir.AluOpType.mult,
            )

        def store(b):
            width = T // STORE_PARTS[b]
            for t in range(0, T, width):
                nc.sync.dma_start(out=out[P * b : P * (b + 1), t : t + width], in_=windows[b % WINDOWS][:, t : t + width])

        start0, start1, start2, start3, end = CHUNKS

        nc.vector.memset(w_plane[:].bitcast(I32), 0)
        load_x(0)
        load_words(0)
        for q in range(P // QUADRANT):
            nc.sync.dma_start(
                out=w_plane[QUADRANT * q : QUADRANT * q + 4, :].bitcast(I32),
                in_=w_scales[0, 4 * q : 4 * q + 4, :].bitcast(I32),
            )
        load_x(1)
        nc.sync.dma_start(offsets[:], offs)
        load_weights(start0, start1)
        load_words(1)
        load_x(2)
        load_weights(start1, start3)
        load_x(3)
        load_x(4)
        load_weights(start3, end)

        nc.vector.memset(windows[0][:], 0.0)
        nc.vector.memset(windows[1][:], 0.0)

        grouped = group_chunk(0, nc.vector.tensor_copy)
        nc.vector.memset(windows[2][:, 0:CLEAR_EARLY], 0.0)
        quantize(0, grouped)
        nc.vector.memset(windows[2][:, CLEAR_EARLY:T], 0.0)
        for b in range(WINDOWS):
            multiply(b, start0, start1, b)

        sums = sums_tile(0, start0, start1)
        fetch(sums[:], 0)
        grouped = grouped_tile(1)
        group(grouped, 1, start1, start1 + VECTOR_SHARE, nc.vector.tensor_copy)
        scatter(0, start0, start1, sums)
        group(grouped, 1, start1 + VECTOR_SHARE, start2, nc.scalar.copy)
        quantize(1, grouped)
        for b in (1, 2):
            sums = sums_tile(b, start0, start1, on=4 * start1 * (b - 1))
            fetch(sums[:], b)
            scatter(b, start0, start1, sums)
        multiply(0, start1, start2, 2)

        quantize(2, group_chunk(2, nc.scalar.copy, on=8 * start1))
        sums = sums_tile(0, start1, start2)
        fetch(sums[:], 2)
        scatter(0, start1, start2, sums)
        multiply(1, start1, start2, 2)
        multiply(1, start2, start3, 1)
        multiply(0, start2, start3, 0)
        multiply(2, 2 * start1, start3, 3, start1)
        multiply(2, start1, 2 * start1, 3)
        multiply(3, start0, start3, 4)
        sums = sums_tile(1, start1, start3)
        fetch(sums[:, 0 : start2 - start1], 2)
        fetch(sums[:, start2 - start1 : start3 - start1], 1)
        scatter(1, start1, start3, sums)

        quantize(3, group_chunk(3, nc.scalar.copy, on="grouped0"))
        sums = sums_tile(2, start1, start3, on="raw4")
        fetch(sums[:], 3)
        scatter(2, start1, start3, sums)
        for b, bank in enumerate((5, 6, 2, 7)):
            multiply(b, start3, end, bank)
        sums = sums_tile(0, start2, end)
        fetch(sums[:, 0 : start3 - start2], 0)
        fetch(sums[:, start3 - start2 : end - start2], 5)
        scatter(0, start2, end, sums)
        store(0)
        for b, bank in ((1, 6), (2, 2)):
            sums = sums_tile(b, start3, end)
            fetch(sums[:], bank)
            scatter(b, start3, end, sums)
            store(b)
        sums = sums_tile(3, start0, end, on=f"sums1_{start3}")
        fetch(sums[:, 0:BANK], 4)
        fetch(sums[:, BANK:S], 7)
        scatter(3, start0, end, sums)
        store(3)
